import numpy as np
import ml_dtypes


def mxq(x, axis, fmt="e4m3"):
    dtype, down = {"e4m3": (ml_dtypes.float8_e4m3fn, 7), "e5m2": (ml_dtypes.float8_e5m2, 14)}[fmt]
    v = np.moveaxis(np.asarray(x, np.float32).astype(ml_dtypes.bfloat16).astype(np.float64), axis, -1)
    blocks = v.reshape(v.shape[:-1] + (-1, 32))
    amax = np.abs(blocks).max(-1, keepdims=True)
    byte = np.maximum(np.where(amax > 0, np.frexp(amax)[1] - 1 + 127, 0) - down, 1)
    scale = np.exp2(byte - 127.0)
    codes = (blocks / scale).astype(np.float32).astype(dtype).astype(np.float64)
    return np.moveaxis((codes * scale).reshape(v.shape), -1, axis)


WIDE = False


def mx_kscale(k):
    if not WIDE:
        return np.ones(k)
    levels = np.array([10, -10, 5, -5, 0])
    if k % 512:
        return np.exp2(np.random.permutation(np.resize(levels, k // 32))).repeat(32)
    a = np.empty((k // 512, 16))
    for p in range(k // 512):
        a[p, :8] = np.random.permutation(np.resize(levels, 8))
        for g in range(8):
            far = levels[np.abs(levels - a[p, g]) >= 10]
            a[p, g + 8] = far[np.random.randint(len(far))]
    return np.exp2(a.ravel()).repeat(32)


def f64(x):
    return np.asarray(x).astype(np.float64)


E2M1 = np.array([0.0, 0.5, 1.0, 1.5, 2.0, 3.0, 4.0, 6.0, -0.0, -0.5, -1.0, -1.5, -2.0, -3.0, -4.0, -6.0])


def pack_weight(w, fmt):
    k, n = w.shape
    w = f64(np.asarray(w, np.float32).astype(ml_dtypes.bfloat16)).reshape(k // 32, 32, n)
    amax = np.abs(w).max(1)
    if fmt == "e4m3":
        byte = np.frexp(amax)[1] - 1 + 127 - 7
    else:
        mant, ex = np.frexp(amax / 6.0)
        byte = np.where(mant > 0.5, ex, ex - 1) + 127
    byte = np.clip(np.where(amax > 0, byte, 1), 1, 254)
    scaled = (w * np.exp2(127.0 - byte)[:, None, :]).reshape(k, n).astype(np.float32)
    by_word = np.ascontiguousarray(scaled.reshape(k // 512, 128, 4, n).transpose(0, 1, 3, 2))
    if fmt == "e4m3":
        words = by_word.astype(ml_dtypes.float8_e4m3fn).view(np.uint8)
    else:
        c = by_word.astype(ml_dtypes.float4_e2m1fn).view(np.uint8) & 0xF
        words = (c[..., 0::2] | (c[..., 1::2] << 4)).reshape(k // 512, 128, 2 * n)
    return np.ascontiguousarray(words), np.ascontiguousarray(byte.astype(np.uint8).reshape(k // 512, 16, n))


def unpack_weight(words, scales, fmt):
    g, _, n = scales.shape
    words = np.ascontiguousarray(words).reshape(g, 128, n, -1)
    if fmt == "e4m3":
        vals = words.view(ml_dtypes.float8_e4m3fn).astype(np.float64)
    else:
        nib = np.empty((g, 128, n, 4), np.uint8)
        nib[..., 0::2] = words & 0xF
        nib[..., 1::2] = words >> 4
        vals = E2M1[nib]
    vals = vals * np.repeat(np.exp2(scales.astype(np.float64) - 127.0), 8, axis=1)[..., None]
    return vals.transpose(0, 1, 3, 2).reshape(g * 512, n)


def silu(v):
    return v / (1.0 + np.exp(-np.maximum(v, -700.0)))


K, M, T = 1536, 1536, 512


def setup_inputs():
    n = np.random.standard_normal
    s = mx_kscale(K)[:, None]
    p_w4 = pack_weight(n((K, M)) / np.sqrt(K) / s, "e2m1")
    p_w8 = pack_weight(n((K, M)) / np.sqrt(K) / s, "e4m3")
    return {
        "x": (n((K, T)) * s).astype(np.float32),
        "w4_words": p_w4[0],
        "w4_scales": p_w4[1],
        "w8_words": p_w8[0],
        "w8_scales": p_w8[1],
        "r": (n((1536, 512))).astype(np.float32),
    }


def reference(x, w4_words, w4_scales, w8_words, w8_scales, r):
    x_ = mxq(f64(x), 0, "e4m3")
    w4_ = unpack_weight(w4_words, w4_scales, "e2m1")
    w8_ = unpack_weight(w8_words, w8_scales, "e4m3")
    y = w4_.T @ x_
    u = w8_.T @ x_
    y = silu(y) * u
    return f64(r) + y

@@ -1,0 +1,147 @@
+from contextlib import ExitStack
+
+import concourse.mybir as mybir
+
+K, M, T = 1536, 1536, 512
+FLOPS = 2 * 2 * K * M * T
+
+F32 = mybir.dt.float32
+BF16 = mybir.dt.bfloat16
+I32 = mybir.dt.int32
+U32 = mybir.dt.uint32
+U8 = mybir.dt.uint8
+FP8X4 = mybir.dt.float8_e4m3fn_x4
+FP4X4 = mybir.dt.float4_e2m1fn_x4
+SILU = mybir.ActivationFunctionType.Silu
+ALU = mybir.AluOpType
+
+P = 128
+PACK = 4
+PASSES = K // (P * PACK)
+TILES = M // P
+HALF = M // 2
+OPEN_TILES = 4
+DVE_COLS = 320
+W8_ROW0 = 4
+PAIR = 2
+ADD_LAG = 5
+
+
+def tile_mix_glu48_fm_res_kernel(tc, x, w4_words, w4_scales, w8_words, w8_scales, r, out):
+    nc = tc.nc
+    with ExitStack() as ctx:
+        keep = ctx.enter_context(tc.tile_pool(name="keep", bufs=1))
+        work = ctx.enter_context(tc.tile_pool(name="work", bufs=3))
+        psum = ctx.enter_context(tc.psum_pool(name="psum", bufs=OPEN_TILES))
+        ctx.enter_context(tc.manual_schedule())
+
+        s4 = keep.tile([P, PASSES, M], U8, name="s4", align_bytes=64)
+        s8 = keep.tile([P, PASSES, M], U8, name="s8", align_bytes=64)
+        warm_in = keep.tile([P, 8], F32, name="warm_in")
+        warm_out = keep.tile([P, 8], F32, name="warm_out")
+        nc.vector.memset(warm_in[:], 0.0)
+        nc.vector.memset(s4[:].rearrange("p a n -> p (a n)").bitcast(I32), 0)
+        nc.vector.memset(s8[:].rearrange("p a n -> p (a n)").bitcast(I32), 0)
+        nc.scalar.activation(out=warm_out[:], in_=warm_in[:], func=SILU)
+
+        for plane, row0, scales in ((s4, 0, w4_scales), (s8, W8_ROW0, w8_scales)):
+            by_row = scales.rearrange("a (q i) n -> i q a n", i=4)
+            for i in range(4):
+                nc.gpsimd.dma_start(out=plane[row0 + i : P : 32, :, :].bitcast(I32), in_=by_row[i].bitcast(I32))
+
+        w4_hbm = w4_words.rearrange("a p b -> p a b")
+        w8_hbm = w8_words.rearrange("a p n t -> p a (n t)")
+        w4 = [keep.tile([P, PASSES, 2 * HALF], U8, name="w4_%d" % h, align_bytes=64) for h in range(2)]
+        w8 = [keep.tile([P, PASSES, HALF], U32, name="w8_%d" % h, align_bytes=64) for h in range(2)]
+        raw = [keep.tile([P, PACK, T], F32, name="raw_%d" % a) for a in range(PASSES)]
+        res = [keep.tile([P, PAIR, T], F32, name="res_%d" % c) for c in range(TILES // PAIR)]
+        gated = [keep.tile([P, PAIR, T], F32, name="gated_%d" % c) for c in range(TILES // PAIR)]
+
+        for a in range(PASSES):
+            nc.sync.dma_start(out=raw[a][:], in_=x[a * P * PACK : (a + 1) * P * PACK, :].rearrange("(p j) t -> p j t", j=PACK))
+            nc.sync.dma_start(out=w4[0][:, a, :].bitcast(I32), in_=w4_hbm[:, a, 0 : 2 * HALF].bitcast(I32))
+            nc.sync.dma_start(out=w8[0][:, a, :].bitcast(I32), in_=w8_hbm[:, a, 0 : 4 * HALF].bitcast(I32))
+        nc.sync.dma_start(out=w4[1][:].bitcast(I32), in_=w4_hbm[:, :, 2 * HALF :].bitcast(I32))
+        nc.sync.dma_start(out=w8[1][:].bitcast(I32), in_=w8_hbm[:, :, 4 * HALF :].bitcast(I32))
+        r_pairs = r.rearrange("(c e p) t -> c p e t", e=PAIR, p=P)
+        out_pairs = out.rearrange("(c e p) t -> c p e t", e=PAIR, p=P)
+        for c in range(TILES // PAIR):
+            nc.sync.dma_start(out=res[c][:], in_=r_pairs[c])
+
+        x_codes = [keep.tile([P, T], U32, name="x_codes_%d" % a, align_bytes=64) for a in range(PASSES)]
+        x_scales = [keep.tile([P, T], U8, name="x_scales_%d" % a, align_bytes=64) for a in range(PASSES)]
+
+        def quantize_pass(a):
+            grouped = keep.tile([P, T, PACK], BF16, name="grouped_%d" % a, align_bytes=64)
+            dst = grouped[:].rearrange("p (c i) j -> p c j i", i=4)
+            src = raw[a][:].rearrange("p j (c i) -> p c j i", i=4)
+            nc.vector.tensor_copy(out=dst[:, : DVE_COLS // 4], in_=src[:, : DVE_COLS // 4])
+            nc.scalar.copy(out=dst[:, DVE_COLS // 4 :], in_=src[:, DVE_COLS // 4 :])
+            nc.vector.quantize_mx(
+                out=x_codes[a][:].bitcast(FP8X4),
+                scales=x_scales[a][:],
+                in_=grouped[:].rearrange("p t j -> p (t j)"),
+            )
+
+        g_acc = {}
+        u_acc = {}
+
+        def gate_pass(n, a):
+            if a == 0:
+                g_acc[n] = psum.tile([P, T], F32, name="g_acc", tag="g_acc")
+            h, c0 = divmod(n * P, HALF)
+            nc.tensor.matmul_mx(
+                out=g_acc[n][:],
+                lhsT=w4[h][:, a, 2 * c0 : 2 * (c0 + P)].bitcast(FP4X4),
+                lhsT_scale=s4[:, a, n * P : (n + 1) * P],
+                rhs=x_codes[a][:].bitcast(FP8X4),
+                rhs_scale=x_scales[a][:],
+                start=(a == 0),
+                stop=(a == PASSES - 1),
+            )
+
+        def up_pass(n, a):
+            if a == 0:
+                u_acc[n] = psum.tile([P, T], F32, name="u_acc", tag="u_acc")
+            h, c0 = divmod(n * P, HALF)
+            nc.tensor.matmul_mx(
+                out=u_acc[n][:],
+                lhsT=w8[h][:, a, c0 : c0 + P].bitcast(FP8X4),
+                lhsT_scale=s8[W8_ROW0:P, a, n * P : (n + 1) * P],
+                rhs=x_codes[a][:].bitcast(FP8X4),
+                rhs_scale=x_scales[a][:],
+                start=(a == 0),
+                stop=(a == PASSES - 1),
+            )
+
+        def add_and_store(c, tiles):
+            nc.vector.tensor_tensor(out=res[c][:, tiles, :], in0=gated[c][:, tiles, :], in1=res[c][:, tiles, :], op=ALU.add)
+            nc.sync.dma_start(out=out_pairs[c][:, tiles, :], in_=res[c][:, tiles, :])
+
+        def finish(n):
+            c, e = divmod(n, PAIR)
+            act = work.tile([P, T], F32, name="act", tag="act")
+            nc.scalar.activation(out=act[:], in_=g_acc[n][:], func=SILU)
+            nc.vector.tensor_tensor(out=gated[c][:, e, :], in0=u_acc[n][:], in1=act[:], op=ALU.mult)
+            if c == TILES // PAIR - 1:
+                add_and_store(c, slice(e, e + 1))
+            elif n >= ADD_LAG:
+                add_and_store(n - ADD_LAG, slice(0, PAIR))
+
+        for a in range(PASSES - 1):
+            quantize_pass(a)
+            for n in range(OPEN_TILES):
+                gate_pass(n, a)
+            for n in range(OPEN_TILES):
+                up_pass(n, a)
+        quantize_pass(PASSES - 1)
+        for n in range(OPEN_TILES):
+            gate_pass(n, PASSES - 1)
+            up_pass(n, PASSES - 1)
+            finish(n)
+        for n in range(OPEN_TILES, TILES):
+            for a in range(PASSES):
+                gate_pass(n, a)
+            for a in range(PASSES):
+                up_pass(n, a)
+            finish(n)

@@ -24,7 +24,8 @@ OPEN_TILES = 4
 DVE_COLS = 320
 W8_ROW0 = 4
 PAIR = 2
-ADD_LAG = 5
+FIRST_ADD = 4
+HEAD = OPEN_TILES * P
 
 
 def tile_mix_glu48_fm_res_kernel(tc, x, w4_words, w4_scales, w8_words, w8_scales, r, out):
@@ -35,19 +36,23 @@ def tile_mix_glu48_fm_res_kernel(tc, x, w4_words, w4_scales, w8_words, w8_scales
         psum = ctx.enter_context(tc.psum_pool(name="psum", bufs=OPEN_TILES))
         ctx.enter_context(tc.manual_schedule())
 
-        s4 = keep.tile([P, PASSES, M], U8, name="s4", align_bytes=64)
+        s4_head = keep.tile([P, PASSES, HEAD], U8, name="s4_head", align_bytes=64)
+        s4_rest = keep.tile([P, PASSES, M - HEAD], U8, name="s4_rest", align_bytes=64)
         s8 = keep.tile([P, PASSES, M], U8, name="s8", align_bytes=64)
         warm_in = keep.tile([P, 8], F32, name="warm_in")
         warm_out = keep.tile([P, 8], F32, name="warm_out")
+        for plane in (s8, s4_head, s4_rest):
+            nc.vector.memset(plane[:].rearrange("p a n -> p (a n)").bitcast(I32), 0)
         nc.vector.memset(warm_in[:], 0.0)
-        nc.vector.memset(s4[:].rearrange("p a n -> p (a n)").bitcast(I32), 0)
-        nc.vector.memset(s8[:].rearrange("p a n -> p (a n)").bitcast(I32), 0)
         nc.scalar.activation(out=warm_out[:], in_=warm_in[:], func=SILU)
 
-        for plane, row0, scales in ((s4, 0, w4_scales), (s8, W8_ROW0, w8_scales)):
+        def load_scales(queue, plane, row0, scales):
             by_row = scales.rearrange("a (q i) n -> i q a n", i=4)
             for i in range(4):
-                nc.gpsimd.dma_start(out=plane[row0 + i : P : 32, :, :].bitcast(I32), in_=by_row[i].bitcast(I32))
+                queue.dma_start(out=plane[row0 + i : P : 32, :, :].bitcast(I32), in_=by_row[i].bitcast(I32))
+
+        load_scales(nc.gpsimd, s8, W8_ROW0, w8_scales)
+        load_scales(nc.gpsimd, s4_rest, 0, w4_scales[:, :, HEAD:])
 
         w4_hbm = w4_words.rearrange("a p b -> p a b")
         w8_hbm = w8_words.rearrange("a p n t -> p a (n t)")
@@ -59,13 +64,16 @@ def tile_mix_glu48_fm_res_kernel(tc, x, w4_words, w4_scales, w8_words, w8_scales
 
         for a in range(PASSES):
             nc.sync.dma_start(out=raw[a][:], in_=x[a * P * PACK : (a + 1) * P * PACK, :].rearrange("(p j) t -> p j t", j=PACK))
+            if a == 0:
+                load_scales(nc.sync, s4_head, 0, w4_scales[:, :, :HEAD])
             nc.sync.dma_start(out=w4[0][:, a, :].bitcast(I32), in_=w4_hbm[:, a, 0 : 2 * HALF].bitcast(I32))
             nc.sync.dma_start(out=w8[0][:, a, :].bitcast(I32), in_=w8_hbm[:, a, 0 : 4 * HALF].bitcast(I32))
-        nc.sync.dma_start(out=w4[1][:].bitcast(I32), in_=w4_hbm[:, :, 2 * HALF :].bitcast(I32))
-        nc.sync.dma_start(out=w8[1][:].bitcast(I32), in_=w8_hbm[:, :, 4 * HALF :].bitcast(I32))
         r_pairs = r.rearrange("(c e p) t -> c p e t", e=PAIR, p=P)
         out_pairs = out.rearrange("(c e p) t -> c p e t", e=PAIR, p=P)
-        for c in range(TILES // PAIR):
+        nc.sync.dma_start(out=w4[1][:].bitcast(I32), in_=w4_hbm[:, :, 2 * HALF :].bitcast(I32))
+        nc.sync.dma_start(out=res[0][:], in_=r_pairs[0])
+        nc.sync.dma_start(out=w8[1][:].bitcast(I32), in_=w8_hbm[:, :, 4 * HALF :].bitcast(I32))
+        for c in range(1, TILES // PAIR):
             nc.sync.dma_start(out=res[c][:], in_=r_pairs[c])
 
         x_codes = [keep.tile([P, T], U32, name="x_codes_%d" % a, align_bytes=64) for a in range(PASSES)]
@@ -75,8 +83,11 @@ def tile_mix_glu48_fm_res_kernel(tc, x, w4_words, w4_scales, w8_words, w8_scales
             grouped = keep.tile([P, T, PACK], BF16, name="grouped_%d" % a, align_bytes=64)
             dst = grouped[:].rearrange("p (c i) j -> p c j i", i=4)
             src = raw[a][:].rearrange("p j (c i) -> p c j i", i=4)
-            nc.vector.tensor_copy(out=dst[:, : DVE_COLS // 4], in_=src[:, : DVE_COLS // 4])
-            nc.scalar.copy(out=dst[:, DVE_COLS // 4 :], in_=src[:, DVE_COLS // 4 :])
+            if a == PASSES - 1:
+                nc.vector.tensor_copy(out=dst[:, : DVE_COLS // 4], in_=src[:, : DVE_COLS // 4])
+                nc.scalar.copy(out=dst[:, DVE_COLS // 4 :], in_=src[:, DVE_COLS // 4 :])
+            else:
+                nc.scalar.copy(out=dst, in_=src)
             nc.vector.quantize_mx(
                 out=x_codes[a][:].bitcast(FP8X4),
                 scales=x_scales[a][:],
@@ -90,58 +101,69 @@ def tile_mix_glu48_fm_res_kernel(tc, x, w4_words, w4_scales, w8_words, w8_scales
             if a == 0:
                 g_acc[n] = psum.tile([P, T], F32, name="g_acc", tag="g_acc")
             h, c0 = divmod(n * P, HALF)
+            plane, s0 = (s4_head, n * P) if n < OPEN_TILES else (s4_rest, n * P - HEAD)
             nc.tensor.matmul_mx(
                 out=g_acc[n][:],
                 lhsT=w4[h][:, a, 2 * c0 : 2 * (c0 + P)].bitcast(FP4X4),
-                lhsT_scale=s4[:, a, n * P : (n + 1) * P],
+                lhsT_scale=plane[:, a, s0 : s0 + P],
                 rhs=x_codes[a][:].bitcast(FP8X4),
                 rhs_scale=x_scales[a][:],
                 start=(a == 0),
                 stop=(a == PASSES - 1),
             )
 
-        def up_pass(n, a):
+        def up_pass(n, a, cols):
             if a == 0:
-                u_acc[n] = psum.tile([P, T], F32, name="u_acc", tag="u_acc")
+                u_acc[n, cols.start] = psum.tile([P, T], F32, name="u_acc", tag="u_acc")
             h, c0 = divmod(n * P, HALF)
             nc.tensor.matmul_mx(
-                out=u_acc[n][:],
+                out=u_acc[n, cols.start][:, cols],
                 lhsT=w8[h][:, a, c0 : c0 + P].bitcast(FP8X4),
                 lhsT_scale=s8[W8_ROW0:P, a, n * P : (n + 1) * P],
-                rhs=x_codes[a][:].bitcast(FP8X4),
-                rhs_scale=x_scales[a][:],
+                rhs=x_codes[a][:, cols].bitcast(FP8X4),
+                rhs_scale=x_scales[a][:, cols],
                 start=(a == 0),
                 stop=(a == PASSES - 1),
             )
 
-        def add_and_store(c, tiles):
-            nc.vector.tensor_tensor(out=res[c][:, tiles, :], in0=gated[c][:, tiles, :], in1=res[c][:, tiles, :], op=ALU.add)
-            nc.sync.dma_start(out=out_pairs[c][:, tiles, :], in_=res[c][:, tiles, :])
-
-        def finish(n):
+        def gate_and_multiply(n, parts):
             c, e = divmod(n, PAIR)
             act = work.tile([P, T], F32, name="act", tag="act")
             nc.scalar.activation(out=act[:], in_=g_acc[n][:], func=SILU)
-            nc.vector.tensor_tensor(out=gated[c][:, e, :], in0=u_acc[n][:], in1=act[:], op=ALU.mult)
-            if c == TILES // PAIR - 1:
-                add_and_store(c, slice(e, e + 1))
-            elif n >= ADD_LAG:
-                add_and_store(n - ADD_LAG, slice(0, PAIR))
+            for cols in parts:
+                nc.vector.tensor_tensor(
+                    out=gated[c][:, e, cols], in0=u_acc[n, cols.start][:, cols], in1=act[:, cols], op=ALU.mult
+                )
+
+        def add_and_store(c, tiles, cols):
+            nc.vector.tensor_tensor(
+                out=res[c][:, tiles, cols], in0=gated[c][:, tiles, cols], in1=res[c][:, tiles, cols], op=ALU.add
+            )
+            nc.sync.dma_start(out=out_pairs[c][:, tiles, cols], in_=res[c][:, tiles, cols])
+
+        whole = slice(0, T)
+        halves = [slice(0, T // 2), slice(T // 2, T)]
+        last_pair = TILES // PAIR - 1
+        add_after = {max(FIRST_ADD + c, PAIR * c + 1): c for c in range(last_pair)}
 
         for a in range(PASSES - 1):
             quantize_pass(a)
             for n in range(OPEN_TILES):
                 gate_pass(n, a)
             for n in range(OPEN_TILES):
-                up_pass(n, a)
+                up_pass(n, a, whole)
         quantize_pass(PASSES - 1)
-        for n in range(OPEN_TILES):
-            gate_pass(n, PASSES - 1)
-            up_pass(n, PASSES - 1)
-            finish(n)
-        for n in range(OPEN_TILES, TILES):
-            for a in range(PASSES):
+        for n in range(TILES):
+            parts = halves if n == TILES - 1 else [whole]
+            todo = range(PASSES - 1, PASSES) if n < OPEN_TILES else range(PASSES)
+            for a in todo:
                 gate_pass(n, a)
-            for a in range(PASSES):
-                up_pass(n, a)
-            finish(n)
+            for cols in parts:
+                for a in todo:
+                    up_pass(n, a, cols)
+            gate_and_multiply(n, parts)
+            if n in add_after:
+                add_and_store(add_after[n], slice(0, PAIR), whole)
+            if n // PAIR == last_pair:
+                for cols in parts:
+                    add_and_store(last_pair, slice(n % PAIR, n % PAIR + 1), cols)

@@ -19,17 +19,18 @@ P = 128
 PACK = 4
 PASSES = K // (P * PACK)
 TILES = M // P
-HALF = M // 2
 OPEN_TILES = 4
 DVE_COLS = 320
 W8_ROW0 = 4
 PAIR = 2
-FIRST_ADD = 4
+ADD_LAG = 5
 HEAD = OPEN_TILES * P
 
 
 def tile_mix_glu48_fm_res_kernel(tc, x, w4_words, w4_scales, w8_words, w8_scales, r, out):
     nc = tc.nc
+    whole = slice(0, T)
+    halves = [slice(0, T // 2), slice(T // 2, T)]
     with ExitStack() as ctx:
         keep = ctx.enter_context(tc.tile_pool(name="keep", bufs=1))
         work = ctx.enter_context(tc.tile_pool(name="work", bufs=3))
@@ -56,8 +57,10 @@ def tile_mix_glu48_fm_res_kernel(tc, x, w4_words, w4_scales, w8_words, w8_scales
 
         w4_hbm = w4_words.rearrange("a p b -> p a b")
         w8_hbm = w8_words.rearrange("a p n t -> p a (n t)")
-        w4 = [keep.tile([P, PASSES, 2 * HALF], U8, name="w4_%d" % h, align_bytes=64) for h in range(2)]
-        w8 = [keep.tile([P, PASSES, HALF], U32, name="w8_%d" % h, align_bytes=64) for h in range(2)]
+        w4_head = keep.tile([P, PASSES, 2 * HEAD], U8, name="w4_head", align_bytes=64)
+        w4_rest = keep.tile([P, PASSES, 2 * (M - HEAD)], U8, name="w4_rest", align_bytes=64)
+        w8_head = keep.tile([P, PASSES, HEAD], U32, name="w8_head", align_bytes=64)
+        w8_rest = keep.tile([P, PASSES, M - HEAD], U32, name="w8_rest", align_bytes=64)
         raw = [keep.tile([P, PACK, T], F32, name="raw_%d" % a) for a in range(PASSES)]
         res = [keep.tile([P, PAIR, T], F32, name="res_%d" % c) for c in range(TILES // PAIR)]
         gated = [keep.tile([P, PAIR, T], F32, name="gated_%d" % c) for c in range(TILES // PAIR)]
@@ -66,14 +69,13 @@ def tile_mix_glu48_fm_res_kernel(tc, x, w4_words, w4_scales, w8_words, w8_scales
             nc.sync.dma_start(out=raw[a][:], in_=x[a * P * PACK : (a + 1) * P * PACK, :].rearrange("(p j) t -> p j t", j=PACK))
             if a == 0:
                 load_scales(nc.sync, s4_head, 0, w4_scales[:, :, :HEAD])
-            nc.sync.dma_start(out=w4[0][:, a, :].bitcast(I32), in_=w4_hbm[:, a, 0 : 2 * HALF].bitcast(I32))
-            nc.sync.dma_start(out=w8[0][:, a, :].bitcast(I32), in_=w8_hbm[:, a, 0 : 4 * HALF].bitcast(I32))
+            nc.sync.dma_start(out=w4_head[:, a, :].bitcast(I32), in_=w4_hbm[:, a, : 2 * HEAD].bitcast(I32))
+            nc.sync.dma_start(out=w8_head[:, a, :].bitcast(I32), in_=w8_hbm[:, a, : 4 * HEAD].bitcast(I32))
         r_pairs = r.rearrange("(c e p) t -> c p e t", e=PAIR, p=P)
         out_pairs = out.rearrange("(c e p) t -> c p e t", e=PAIR, p=P)
-        nc.sync.dma_start(out=w4[1][:].bitcast(I32), in_=w4_hbm[:, :, 2 * HALF :].bitcast(I32))
-        nc.sync.dma_start(out=res[0][:], in_=r_pairs[0])
-        nc.sync.dma_start(out=w8[1][:].bitcast(I32), in_=w8_hbm[:, :, 4 * HALF :].bitcast(I32))
-        for c in range(1, TILES // PAIR):
+        nc.sync.dma_start(out=w4_rest[:].bitcast(I32), in_=w4_hbm[:, :, 2 * HEAD :].bitcast(I32))
+        nc.sync.dma_start(out=w8_rest[:].bitcast(I32), in_=w8_hbm[:, :, 4 * HEAD :].bitcast(I32))
+        for c in range(TILES // PAIR):
             nc.sync.dma_start(out=res[c][:], in_=r_pairs[c])
 
         x_codes = [keep.tile([P, T], U32, name="x_codes_%d" % a, align_bytes=64) for a in range(PASSES)]
@@ -83,16 +85,15 @@ def tile_mix_glu48_fm_res_kernel(tc, x, w4_words, w4_scales, w8_words, w8_scales
             grouped = keep.tile([P, T, PACK], BF16, name="grouped_%d" % a, align_bytes=64)
             dst = grouped[:].rearrange("p (c i) j -> p c j i", i=4)
             src = raw[a][:].rearrange("p j (c i) -> p c j i", i=4)
-            if a == PASSES - 1:
-                nc.vector.tensor_copy(out=dst[:, : DVE_COLS // 4], in_=src[:, : DVE_COLS // 4])
-                nc.scalar.copy(out=dst[:, DVE_COLS // 4 :], in_=src[:, DVE_COLS // 4 :])
-            else:
-                nc.scalar.copy(out=dst, in_=src)
-            nc.vector.quantize_mx(
-                out=x_codes[a][:].bitcast(FP8X4),
-                scales=x_scales[a][:],
-                in_=grouped[:].rearrange("p t j -> p (t j)"),
-            )
+            nc.vector.tensor_copy(out=dst[:, : T // 8], in_=src[:, : T // 8])
+            nc.vector.tensor_copy(out=dst[:, T // 8 : DVE_COLS // 4], in_=src[:, T // 8 : DVE_COLS // 4])
+            nc.scalar.copy(out=dst[:, DVE_COLS // 4 :], in_=src[:, DVE_COLS // 4 :])
+            for cols in halves:
+                nc.vector.quantize_mx(
+                    out=x_codes[a][:, cols].bitcast(FP8X4),
+                    scales=x_scales[a][:, cols],
+                    in_=grouped[:, cols, :].rearrange("p t j -> p (t j)"),
+                )
 
         g_acc = {}
         u_acc = {}
@@ -100,12 +101,11 @@ def tile_mix_glu48_fm_res_kernel(tc, x, w4_words, w4_scales, w8_words, w8_scales
         def gate_pass(n, a):
             if a == 0:
                 g_acc[n] = psum.tile([P, T], F32, name="g_acc", tag="g_acc")
-            h, c0 = divmod(n * P, HALF)
-            plane, s0 = (s4_head, n * P) if n < OPEN_TILES else (s4_rest, n * P - HEAD)
+            words, plane, c0 = (w4_head, s4_head, n * P) if n < OPEN_TILES else (w4_rest, s4_rest, n * P - HEAD)
             nc.tensor.matmul_mx(
                 out=g_acc[n][:],
-                lhsT=w4[h][:, a, 2 * c0 : 2 * (c0 + P)].bitcast(FP4X4),
-                lhsT_scale=plane[:, a, s0 : s0 + P],
+                lhsT=words[:, a, 2 * c0 : 2 * (c0 + P)].bitcast(FP4X4),
+                lhsT_scale=plane[:, a, c0 : c0 + P],
                 rhs=x_codes[a][:].bitcast(FP8X4),
                 rhs_scale=x_scales[a][:],
                 start=(a == 0),
@@ -115,10 +115,10 @@ def tile_mix_glu48_fm_res_kernel(tc, x, w4_words, w4_scales, w8_words, w8_scales
         def up_pass(n, a, cols):
             if a == 0:
                 u_acc[n, cols.start] = psum.tile([P, T], F32, name="u_acc", tag="u_acc")
-            h, c0 = divmod(n * P, HALF)
+            words, c0 = (w8_head, n * P) if n < OPEN_TILES else (w8_rest, n * P - HEAD)
             nc.tensor.matmul_mx(
                 out=u_acc[n, cols.start][:, cols],
-                lhsT=w8[h][:, a, c0 : c0 + P].bitcast(FP8X4),
+                lhsT=words[:, a, c0 : c0 + P].bitcast(FP8X4),
                 lhsT_scale=s8[W8_ROW0:P, a, n * P : (n + 1) * P],
                 rhs=x_codes[a][:, cols].bitcast(FP8X4),
                 rhs_scale=x_scales[a][:, cols],
@@ -141,10 +141,7 @@ def tile_mix_glu48_fm_res_kernel(tc, x, w4_words, w4_scales, w8_words, w8_scales
             )
             nc.sync.dma_start(out=out_pairs[c][:, tiles, cols], in_=res[c][:, tiles, cols])
 
-        whole = slice(0, T)
-        halves = [slice(0, T // 2), slice(T // 2, T)]
         last_pair = TILES // PAIR - 1
-        add_after = {max(FIRST_ADD + c, PAIR * c + 1): c for c in range(last_pair)}
 
         for a in range(PASSES - 1):
             quantize_pass(a)
@@ -153,17 +150,19 @@ def tile_mix_glu48_fm_res_kernel(tc, x, w4_words, w4_scales, w8_words, w8_scales
             for n in range(OPEN_TILES):
                 up_pass(n, a, whole)
         quantize_pass(PASSES - 1)
+        gates_before = {OPEN_TILES: [OPEN_TILES, OPEN_TILES + 1], OPEN_TILES + 1: []}
         for n in range(TILES):
             parts = halves if n == TILES - 1 else [whole]
             todo = range(PASSES - 1, PASSES) if n < OPEN_TILES else range(PASSES)
-            for a in todo:
-                gate_pass(n, a)
+            for m in gates_before.get(n, [n]):
+                for a in todo:
+                    gate_pass(m, a)
             for cols in parts:
                 for a in todo:
                     up_pass(n, a, cols)
             gate_and_multiply(n, parts)
-            if n in add_after:
-                add_and_store(add_after[n], slice(0, PAIR), whole)
             if n // PAIR == last_pair:
                 for cols in parts:
                     add_and_store(last_pair, slice(n % PAIR, n % PAIR + 1), cols)
+            elif n >= ADD_LAG:
+                add_and_store(n - ADD_LAG, slice(0, PAIR), whole)

@@ -21,9 +21,8 @@ PASSES = K // (P * PACK)
 TILES = M // P
 OPEN_TILES = 4
 DVE_COLS = 320
-W8_ROW0 = 4
 PAIR = 2
-ADD_LAG = 5
+FIRST_ADD = 4
 HEAD = OPEN_TILES * P
 
 
@@ -37,45 +36,49 @@ def tile_mix_glu48_fm_res_kernel(tc, x, w4_words, w4_scales, w8_words, w8_scales
         psum = ctx.enter_context(tc.psum_pool(name="psum", bufs=OPEN_TILES))
         ctx.enter_context(tc.manual_schedule())
 
-        s4_head = keep.tile([P, PASSES, HEAD], U8, name="s4_head", align_bytes=64)
-        s4_rest = keep.tile([P, PASSES, M - HEAD], U8, name="s4_rest", align_bytes=64)
-        s8 = keep.tile([P, PASSES, M], U8, name="s8", align_bytes=64)
+        w_scales = keep.tile([P, PASSES, M], U8, name="w_scales", align_bytes=64)
         warm_in = keep.tile([P, 8], F32, name="warm_in")
         warm_out = keep.tile([P, 8], F32, name="warm_out")
-        for plane in (s8, s4_head, s4_rest):
-            nc.vector.memset(plane[:].rearrange("p a n -> p (a n)").bitcast(I32), 0)
+        nc.vector.memset(w_scales[:].rearrange("p a n -> p (a n)").bitcast(I32), 0)
         nc.vector.memset(warm_in[:], 0.0)
         nc.scalar.activation(out=warm_out[:], in_=warm_in[:], func=SILU)
-
-        def load_scales(queue, plane, row0, scales):
-            by_row = scales.rearrange("a (q i) n -> i q a n", i=4)
-            for i in range(4):
-                queue.dma_start(out=plane[row0 + i : P : 32, :, :].bitcast(I32), in_=by_row[i].bitcast(I32))
-
-        load_scales(nc.gpsimd, s8, W8_ROW0, w8_scales)
-        load_scales(nc.gpsimd, s4_rest, 0, w4_scales[:, :, HEAD:])
 
         w4_hbm = w4_words.rearrange("a p b -> p a b")
         w8_hbm = w8_words.rearrange("a p n t -> p a (n t)")
         w4_head = keep.tile([P, PASSES, 2 * HEAD], U8, name="w4_head", align_bytes=64)
         w4_rest = keep.tile([P, PASSES, 2 * (M - HEAD)], U8, name="w4_rest", align_bytes=64)
-        w8_head = keep.tile([P, PASSES, HEAD], U32, name="w8_head", align_bytes=64)
-        w8_rest = keep.tile([P, PASSES, M - HEAD], U32, name="w8_rest", align_bytes=64)
+        w8 = [keep.tile([P, PASSES, HEAD], U32, name="w8_%d" % b, align_bytes=64) for b in range(M // HEAD)]
         raw = [keep.tile([P, PACK, T], F32, name="raw_%d" % a) for a in range(PASSES)]
         res = [keep.tile([P, PAIR, T], F32, name="res_%d" % c) for c in range(TILES // PAIR)]
         gated = [keep.tile([P, PAIR, T], F32, name="gated_%d" % c) for c in range(TILES // PAIR)]
 
-        for a in range(PASSES):
-            nc.sync.dma_start(out=raw[a][:], in_=x[a * P * PACK : (a + 1) * P * PACK, :].rearrange("(p j) t -> p j t", j=PACK))
-            if a == 0:
-                load_scales(nc.sync, s4_head, 0, w4_scales[:, :, :HEAD])
+        def load_x(a):
+            rows = x[a * P * PACK : (a + 1) * P * PACK, :]
+            nc.sync.dma_start(out=raw[a][:], in_=rows.rearrange("(p j) t -> p j t", j=PACK))
+
+        def load_head(a):
             nc.sync.dma_start(out=w4_head[:, a, :].bitcast(I32), in_=w4_hbm[:, a, : 2 * HEAD].bitcast(I32))
-            nc.sync.dma_start(out=w8_head[:, a, :].bitcast(I32), in_=w8_hbm[:, a, : 4 * HEAD].bitcast(I32))
+            nc.sync.dma_start(out=w8[0][:, a, :].bitcast(I32), in_=w8_hbm[:, a, : 4 * HEAD].bitcast(I32))
+
+        load_head(0)
+        load_x(0)
+        w4_rows = w4_scales.rearrange("a (q i) n -> i q a n", i=4)
+        for i in range(4):
+            nc.sync.dma_start(out=w_scales[i:P:32, :, :].bitcast(I32), in_=w4_rows[i].bitcast(I32))
+            nc.sync.dma_start(
+                out=w_scales[32 * i + 4 : 32 * i + 4 + 4 * PASSES, 0, :].bitcast(I32),
+                in_=w8_scales[:, 4 * i : 4 * i + 4, :].bitcast(I32),
+            )
+        for a in range(1, PASSES):
+            load_x(a)
+            load_head(a)
         r_pairs = r.rearrange("(c e p) t -> c p e t", e=PAIR, p=P)
         out_pairs = out.rearrange("(c e p) t -> c p e t", e=PAIR, p=P)
         nc.sync.dma_start(out=w4_rest[:].bitcast(I32), in_=w4_hbm[:, :, 2 * HEAD :].bitcast(I32))
-        nc.sync.dma_start(out=w8_rest[:].bitcast(I32), in_=w8_hbm[:, :, 4 * HEAD :].bitcast(I32))
+        nc.sync.dma_start(out=w8[1][:].bitcast(I32), in_=w8_hbm[:, :, 4 * HEAD : 8 * HEAD].bitcast(I32))
         for c in range(TILES // PAIR):
+            if c == 2:
+                nc.sync.dma_start(out=w8[2][:].bitcast(I32), in_=w8_hbm[:, :, 8 * HEAD :].bitcast(I32))
             nc.sync.dma_start(out=res[c][:], in_=r_pairs[c])
 
         x_codes = [keep.tile([P, T], U32, name="x_codes_%d" % a, align_bytes=64) for a in range(PASSES)]
@@ -101,11 +104,11 @@ def tile_mix_glu48_fm_res_kernel(tc, x, w4_words, w4_scales, w8_words, w8_scales
         def gate_pass(n, a):
             if a == 0:
                 g_acc[n] = psum.tile([P, T], F32, name="g_acc", tag="g_acc")
-            words, plane, c0 = (w4_head, s4_head, n * P) if n < OPEN_TILES else (w4_rest, s4_rest, n * P - HEAD)
+            words, c0 = (w4_head, n * P) if n < OPEN_TILES else (w4_rest, n * P - HEAD)
             nc.tensor.matmul_mx(
                 out=g_acc[n][:],
                 lhsT=words[:, a, 2 * c0 : 2 * (c0 + P)].bitcast(FP4X4),
-                lhsT_scale=plane[:, a, c0 : c0 + P],
+                lhsT_scale=w_scales[:, a, n * P : (n + 1) * P],
                 rhs=x_codes[a][:].bitcast(FP8X4),
                 rhs_scale=x_scales[a][:],
                 start=(a == 0),
@@ -115,11 +118,11 @@ def tile_mix_glu48_fm_res_kernel(tc, x, w4_words, w4_scales, w8_words, w8_scales
         def up_pass(n, a, cols):
             if a == 0:
                 u_acc[n, cols.start] = psum.tile([P, T], F32, name="u_acc", tag="u_acc")
-            words, c0 = (w8_head, n * P) if n < OPEN_TILES else (w8_rest, n * P - HEAD)
+            b, c0 = divmod(n * P, HEAD)
             nc.tensor.matmul_mx(
                 out=u_acc[n, cols.start][:, cols],
-                lhsT=words[:, a, c0 : c0 + P].bitcast(FP8X4),
-                lhsT_scale=s8[W8_ROW0:P, a, n * P : (n + 1) * P],
+                lhsT=w8[b][:, a, c0 : c0 + P].bitcast(FP8X4),
+                lhsT_scale=w_scales[4 + 4 * a : P, 0, n * P : (n + 1) * P],
                 rhs=x_codes[a][:, cols].bitcast(FP8X4),
                 rhs_scale=x_scales[a][:, cols],
                 start=(a == 0),
@@ -142,6 +145,7 @@ def tile_mix_glu48_fm_res_kernel(tc, x, w4_words, w4_scales, w8_words, w8_scales
             nc.sync.dma_start(out=out_pairs[c][:, tiles, cols], in_=res[c][:, tiles, cols])
 
         last_pair = TILES // PAIR - 1
+        add_after = {max(FIRST_ADD + c, PAIR * c + 1): c for c in range(last_pair)}
 
         for a in range(PASSES - 1):
             quantize_pass(a)
@@ -164,5 +168,5 @@ def tile_mix_glu48_fm_res_kernel(tc, x, w4_words, w4_scales, w8_words, w8_scales
             if n // PAIR == last_pair:
                 for cols in parts:
                     add_and_store(last_pair, slice(n % PAIR, n % PAIR + 1), cols)
-            elif n >= ADD_LAG:
-                add_and_store(n - ADD_LAG, slice(0, PAIR), whole)
+            elif n in add_after:
+                add_and_store(add_after[n], slice(0, PAIR), whole)

@@ -19,11 +19,12 @@ P = 128
 PACK = 4
 PASSES = K // (P * PACK)
 TILES = M // P
-OPEN_TILES = 4
+BANKS = 8
 DVE_COLS = 320
 PAIR = 2
-FIRST_ADD = 4
-HEAD = OPEN_TILES * P
+W8_BLOCK = 6 * P
+R_EDGES = (0, 2, 4, 8, TILES)
+OUT_EDGES = (0, 4, 8, 10)
 
 
 def tile_mix_glu48_fm_res_kernel(tc, x, w4_words, w4_scales, w8_words, w8_scales, r, out):
@@ -32,54 +33,57 @@ def tile_mix_glu48_fm_res_kernel(tc, x, w4_words, w4_scales, w8_words, w8_scales
     halves = [slice(0, T // 2), slice(T // 2, T)]
     with ExitStack() as ctx:
         keep = ctx.enter_context(tc.tile_pool(name="keep", bufs=1))
-        work = ctx.enter_context(tc.tile_pool(name="work", bufs=3))
-        psum = ctx.enter_context(tc.psum_pool(name="psum", bufs=OPEN_TILES))
+        psum = ctx.enter_context(tc.psum_pool(name="psum", bufs=BANKS))
         ctx.enter_context(tc.manual_schedule())
 
         w_scales = keep.tile([P, PASSES, M], U8, name="w_scales", align_bytes=64)
+        w8_planes = keep.tile([P, M], U8, name="w8_planes", align_bytes=64)
         warm_in = keep.tile([P, 8], F32, name="warm_in")
         warm_out = keep.tile([P, 8], F32, name="warm_out")
         nc.vector.memset(w_scales[:].rearrange("p a n -> p (a n)").bitcast(I32), 0)
         nc.vector.memset(warm_in[:], 0.0)
+        nc.vector.memset(w8_planes[:].bitcast(I32), 0)
         nc.scalar.activation(out=warm_out[:], in_=warm_in[:], func=SILU)
 
-        w4_hbm = w4_words.rearrange("a p b -> p a b")
         w8_hbm = w8_words.rearrange("a p n t -> p a (n t)")
-        w4_head = keep.tile([P, PASSES, 2 * HEAD], U8, name="w4_head", align_bytes=64)
-        w4_rest = keep.tile([P, PASSES, 2 * (M - HEAD)], U8, name="w4_rest", align_bytes=64)
-        w8 = [keep.tile([P, PASSES, HEAD], U32, name="w8_%d" % b, align_bytes=64) for b in range(M // HEAD)]
+        w4 = [keep.tile([P, 2 * M], U8, name="w4_%d" % a, align_bytes=64) for a in range(PASSES)]
+        w8 = [keep.tile([P, PASSES, W8_BLOCK], U32, name="w8_%d" % b, align_bytes=64) for b in range(M // W8_BLOCK)]
         raw = [keep.tile([P, PACK, T], F32, name="raw_%d" % a) for a in range(PASSES)]
-        res = [keep.tile([P, PAIR, T], F32, name="res_%d" % c) for c in range(TILES // PAIR)]
-        gated = [keep.tile([P, PAIR, T], F32, name="gated_%d" % c) for c in range(TILES // PAIR)]
+        res = keep.tile([P, TILES, T], F32, name="res")
+        gated = keep.tile([P, TILES, T], F32, name="gated")
+        act = [keep.tile([P, T], F32, name="act_%d" % n) for n in range(TILES)]
+        r_tiles = r.rearrange("(n p) t -> p n t", p=P)
+        out_tiles = out.rearrange("(n p) t -> p n t", p=P)
 
-        def load_x(a):
+        def load_pass(a):
             rows = x[a * P * PACK : (a + 1) * P * PACK, :]
             nc.sync.dma_start(out=raw[a][:], in_=rows.rearrange("(p j) t -> p j t", j=PACK))
+            nc.sync.dma_start(out=w4[a][:].bitcast(I32), in_=w4_words[a].bitcast(I32))
 
-        def load_head(a):
-            nc.sync.dma_start(out=w4_head[:, a, :].bitcast(I32), in_=w4_hbm[:, a, : 2 * HEAD].bitcast(I32))
-            nc.sync.dma_start(out=w8[0][:, a, :].bitcast(I32), in_=w8_hbm[:, a, : 4 * HEAD].bitcast(I32))
+        def load_w8(b):
+            cols = slice(4 * b * W8_BLOCK, 4 * (b + 1) * W8_BLOCK)
+            nc.sync.dma_start(out=w8[b][:].bitcast(I32), in_=w8_hbm[:, :, cols].bitcast(I32))
 
-        load_head(0)
-        load_x(0)
+        def load_r(c):
+            tiles = slice(R_EDGES[c], R_EDGES[c + 1])
+            nc.sync.dma_start(out=res[:, tiles, :], in_=r_tiles[:, tiles, :])
+
+        load_pass(0)
         w4_rows = w4_scales.rearrange("a (q i) n -> i q a n", i=4)
         for i in range(4):
             nc.sync.dma_start(out=w_scales[i:P:32, :, :].bitcast(I32), in_=w4_rows[i].bitcast(I32))
-            nc.sync.dma_start(
-                out=w_scales[32 * i + 4 : 32 * i + 4 + 4 * PASSES, 0, :].bitcast(I32),
-                in_=w8_scales[:, 4 * i : 4 * i + 4, :].bitcast(I32),
-            )
         for a in range(1, PASSES):
-            load_x(a)
-            load_head(a)
-        r_pairs = r.rearrange("(c e p) t -> c p e t", e=PAIR, p=P)
-        out_pairs = out.rearrange("(c e p) t -> c p e t", e=PAIR, p=P)
-        nc.sync.dma_start(out=w4_rest[:].bitcast(I32), in_=w4_hbm[:, :, 2 * HEAD :].bitcast(I32))
-        nc.sync.dma_start(out=w8[1][:].bitcast(I32), in_=w8_hbm[:, :, 4 * HEAD : 8 * HEAD].bitcast(I32))
-        for c in range(TILES // PAIR):
-            if c == 2:
-                nc.sync.dma_start(out=w8[2][:].bitcast(I32), in_=w8_hbm[:, :, 8 * HEAD :].bitcast(I32))
-            nc.sync.dma_start(out=res[c][:], in_=r_pairs[c])
+            load_pass(a)
+        for q in range(4):
+            nc.gpsimd.dma_start(
+                out=w8_planes[32 * q + 4 : 32 * q + 4 + 4 * PASSES, :].bitcast(I32),
+                in_=w8_scales[:, 4 * q : 4 * q + 4, :].bitcast(I32),
+            )
+        load_w8(0)
+        load_r(0)
+        load_w8(1)
+        for c in range(1, len(R_EDGES) - 1):
+            load_r(c)
 
         x_codes = [keep.tile([P, T], U32, name="x_codes_%d" % a, align_bytes=64) for a in range(PASSES)]
         x_scales = [keep.tile([P, T], U8, name="x_scales_%d" % a, align_bytes=64) for a in range(PASSES)]
@@ -103,70 +107,72 @@ def tile_mix_glu48_fm_res_kernel(tc, x, w4_words, w4_scales, w8_words, w8_scales
 
         def gate_pass(n, a):
             if a == 0:
-                g_acc[n] = psum.tile([P, T], F32, name="g_acc", tag="g_acc")
-            words, c0 = (w4_head, n * P) if n < OPEN_TILES else (w4_rest, n * P - HEAD)
+                g_acc[n] = psum.tile([P, T], F32, name="acc", tag="acc")
             nc.tensor.matmul_mx(
                 out=g_acc[n][:],
-                lhsT=words[:, a, 2 * c0 : 2 * (c0 + P)].bitcast(FP4X4),
+                lhsT=w4[a][:, 2 * n * P : 2 * (n + 1) * P].bitcast(FP4X4),
                 lhsT_scale=w_scales[:, a, n * P : (n + 1) * P],
                 rhs=x_codes[a][:].bitcast(FP8X4),
                 rhs_scale=x_scales[a][:],
                 start=(a == 0),
                 stop=(a == PASSES - 1),
             )
+            if a == PASSES - 1:
+                nc.scalar.activation(out=act[n][:], in_=g_acc[n][:], func=SILU)
 
-        def up_pass(n, a, cols):
-            if a == 0:
-                u_acc[n, cols.start] = psum.tile([P, T], F32, name="u_acc", tag="u_acc")
-            b, c0 = divmod(n * P, HEAD)
-            nc.tensor.matmul_mx(
-                out=u_acc[n, cols.start][:, cols],
-                lhsT=w8[b][:, a, c0 : c0 + P].bitcast(FP8X4),
-                lhsT_scale=w_scales[4 + 4 * a : P, 0, n * P : (n + 1) * P],
-                rhs=x_codes[a][:, cols].bitcast(FP8X4),
-                rhs_scale=x_scales[a][:, cols],
-                start=(a == 0),
-                stop=(a == PASSES - 1),
-            )
-
-        def gate_and_multiply(n, parts):
-            c, e = divmod(n, PAIR)
-            act = work.tile([P, T], F32, name="act", tag="act")
-            nc.scalar.activation(out=act[:], in_=g_acc[n][:], func=SILU)
-            for cols in parts:
-                nc.vector.tensor_tensor(
-                    out=gated[c][:, e, cols], in0=u_acc[n, cols.start][:, cols], in1=act[:, cols], op=ALU.mult
+        def up_product(n, cols):
+            acc = psum.tile([P, T], F32, name="acc", tag="acc")
+            u_acc[n, cols.start] = acc
+            b, c0 = divmod(n * P, W8_BLOCK)
+            for a in range(PASSES):
+                nc.tensor.matmul_mx(
+                    out=acc[:, cols],
+                    lhsT=w8[b][:, a, c0 : c0 + P].bitcast(FP8X4),
+                    lhsT_scale=w8_planes[4 + 4 * a : P, n * P : (n + 1) * P],
+                    rhs=x_codes[a][:, cols].bitcast(FP8X4),
+                    rhs_scale=x_scales[a][:, cols],
+                    start=(a == 0),
+                    stop=(a == PASSES - 1),
                 )
 
-        def add_and_store(c, tiles, cols):
+        def multiply(n, cols):
             nc.vector.tensor_tensor(
-                out=res[c][:, tiles, cols], in0=gated[c][:, tiles, cols], in1=res[c][:, tiles, cols], op=ALU.add
+                out=gated[:, n, cols], in0=u_acc[n, cols.start][:, cols], in1=act[n][:, cols], op=ALU.mult
             )
-            nc.sync.dma_start(out=out_pairs[c][:, tiles, cols], in_=res[c][:, tiles, cols])
 
-        last_pair = TILES // PAIR - 1
-        add_after = {max(FIRST_ADD + c, PAIR * c + 1): c for c in range(last_pair)}
+        def add(tiles, cols):
+            nc.vector.tensor_tensor(
+                out=res[:, tiles, cols], in0=gated[:, tiles, cols], in1=res[:, tiles, cols], op=ALU.add
+            )
 
-        for a in range(PASSES - 1):
+        def store(tiles, cols):
+            nc.sync.dma_start(out=out_tiles[:, tiles, cols], in_=res[:, tiles, cols])
+
+        for a in range(PASSES):
             quantize_pass(a)
-            for n in range(OPEN_TILES):
+            for n in range(BANKS):
                 gate_pass(n, a)
-            for n in range(OPEN_TILES):
-                up_pass(n, a, whole)
-        quantize_pass(PASSES - 1)
-        gates_before = {OPEN_TILES: [OPEN_TILES, OPEN_TILES + 1], OPEN_TILES + 1: []}
+        last = TILES - 1
         for n in range(TILES):
-            parts = halves if n == TILES - 1 else [whole]
-            todo = range(PASSES - 1, PASSES) if n < OPEN_TILES else range(PASSES)
-            for m in gates_before.get(n, [n]):
-                for a in todo:
-                    gate_pass(m, a)
+            if n >= BANKS:
+                for a in range(PASSES):
+                    gate_pass(n, a)
+            parts = halves if n == last else [whole]
             for cols in parts:
-                for a in todo:
-                    up_pass(n, a, cols)
-            gate_and_multiply(n, parts)
-            if n // PAIR == last_pair:
+                up_product(n, cols)
+            for cols in parts:
+                multiply(n, cols)
+            if n >= last - 1:
                 for cols in parts:
-                    add_and_store(last_pair, slice(n % PAIR, n % PAIR + 1), cols)
-            elif n in add_after:
-                add_and_store(add_after[n], slice(0, PAIR), whole)
+                    add(slice(n, n + 1), cols)
+                    store(slice(n, n + 1), cols)
+                continue
+            if n == last - 2:
+                done = n + 1
+            elif n >= PAIR and n % PAIR == 0:
+                done = n
+            else:
+                continue
+            add(slice(done - PAIR, done), whole)
+            if done in OUT_EDGES:
+                store(slice(OUT_EDGES[list(OUT_EDGES).index(done) - 1], done), whole)

@@ -21,10 +21,11 @@ PASSES = K // (P * PACK)
 TILES = M // P
 BANKS = 8
 DVE_COLS = 320
-PAIR = 2
-W8_BLOCK = 6 * P
-R_EDGES = (0, 2, 4, 8, TILES)
-OUT_EDGES = (0, 4, 8, 10)
+HEAD = BANKS * P
+W8_EDGES = (0, 2, 6, TILES)
+CLOSE_AHEAD = 3
+STORE_FROM = {4: 0, 8: 4, 10: 8, 11: 10}
+R_EDGES = (0, 2, 4, 6, 8, TILES)
 
 
 def tile_mix_glu48_fm_res_kernel(tc, x, w4_words, w4_scales, w8_words, w8_scales, r, out):
@@ -36,19 +37,31 @@ def tile_mix_glu48_fm_res_kernel(tc, x, w4_words, w4_scales, w8_words, w8_scales
         psum = ctx.enter_context(tc.psum_pool(name="psum", bufs=BANKS))
         ctx.enter_context(tc.manual_schedule())
 
-        w_scales = keep.tile([P, PASSES, M], U8, name="w_scales", align_bytes=64)
+        head_planes = keep.tile([P, PASSES, HEAD], U8, name="head_planes", align_bytes=64)
+        rest_planes = keep.tile([P, PASSES, M - HEAD], U8, name="rest_planes", align_bytes=64)
         w8_planes = keep.tile([P, M], U8, name="w8_planes", align_bytes=64)
         warm_in = keep.tile([P, 8], F32, name="warm_in")
         warm_out = keep.tile([P, 8], F32, name="warm_out")
-        nc.vector.memset(w_scales[:].rearrange("p a n -> p (a n)").bitcast(I32), 0)
+        nc.vector.memset(head_planes[:].rearrange("p a n -> p (a n)").bitcast(I32), 0)
         nc.vector.memset(warm_in[:], 0.0)
         nc.vector.memset(w8_planes[:].bitcast(I32), 0)
+        nc.vector.memset(rest_planes[:].rearrange("p a n -> p (a n)").bitcast(I32), 0)
         nc.scalar.activation(out=warm_out[:], in_=warm_in[:], func=SILU)
 
         w8_hbm = w8_words.rearrange("a p n t -> p a (n t)")
-        w4 = [keep.tile([P, 2 * M], U8, name="w4_%d" % a, align_bytes=64) for a in range(PASSES)]
-        w8 = [keep.tile([P, PASSES, W8_BLOCK], U32, name="w8_%d" % b, align_bytes=64) for b in range(M // W8_BLOCK)]
-        raw = [keep.tile([P, PACK, T], F32, name="raw_%d" % a) for a in range(PASSES)]
+        w4_hbm = w4_words.rearrange("a p b -> p a b")
+        w4_head = [keep.tile([P, 2 * HEAD], U8, name="w4_head_%d" % a, align_bytes=64) for a in range(PASSES)]
+        w4_rest = keep.tile([P, PASSES, 2 * (M - HEAD)], U8, name="w4_rest", align_bytes=64)
+        w8 = [
+            keep.tile([P, PASSES, (hi - lo) * P], U32, name="w8_%d" % lo, align_bytes=64)
+            for lo, hi in zip(W8_EDGES, W8_EDGES[1:])
+        ]
+        x_parts = [[whole]] * (PASSES - 1) + [halves]
+        raw = {
+            (a, cols.start): keep.tile([P, PACK, cols.stop - cols.start], F32, name="raw_%d_%d" % (a, cols.start))
+            for a in range(PASSES)
+            for cols in x_parts[a]
+        }
         res = keep.tile([P, TILES, T], F32, name="res")
         gated = keep.tile([P, TILES, T], F32, name="gated")
         act = [keep.tile([P, T], F32, name="act_%d" % n) for n in range(TILES)]
@@ -57,50 +70,71 @@ def tile_mix_glu48_fm_res_kernel(tc, x, w4_words, w4_scales, w8_words, w8_scales
 
         def load_pass(a):
             rows = x[a * P * PACK : (a + 1) * P * PACK, :]
-            nc.sync.dma_start(out=raw[a][:], in_=rows.rearrange("(p j) t -> p j t", j=PACK))
-            nc.sync.dma_start(out=w4[a][:].bitcast(I32), in_=w4_words[a].bitcast(I32))
+            for cols in x_parts[a]:
+                nc.sync.dma_start(out=raw[a, cols.start][:], in_=rows.rearrange("(p j) t -> p j t", j=PACK)[:, :, cols])
+            nc.sync.dma_start(out=w4_head[a][:].bitcast(I32), in_=w4_hbm[:, a, : 2 * HEAD].bitcast(I32))
 
         def load_w8(b):
-            cols = slice(4 * b * W8_BLOCK, 4 * (b + 1) * W8_BLOCK)
+            cols = slice(4 * P * W8_EDGES[b], 4 * P * W8_EDGES[b + 1])
             nc.sync.dma_start(out=w8[b][:].bitcast(I32), in_=w8_hbm[:, :, cols].bitcast(I32))
 
         def load_r(c):
             tiles = slice(R_EDGES[c], R_EDGES[c + 1])
             nc.sync.dma_start(out=res[:, tiles, :], in_=r_tiles[:, tiles, :])
 
+        def load_w4_planes(queue, planes, cols):
+            rows = w4_scales.rearrange("a (q i) n -> i q a n", i=4)
+            for i in range(4):
+                queue.dma_start(out=planes[i:P:32, :, :].bitcast(I32), in_=rows[i][:, :, cols].bitcast(I32))
+
+        def load_w8_planes(queue):
+            for q in range(4):
+                queue.dma_start(
+                    out=w8_planes[32 * q + 4 : 32 * q + 4 + 4 * PASSES, :].bitcast(I32),
+                    in_=w8_scales[:, 4 * q : 4 * q + 4, :].bitcast(I32),
+                )
+
         load_pass(0)
-        w4_rows = w4_scales.rearrange("a (q i) n -> i q a n", i=4)
-        for i in range(4):
-            nc.sync.dma_start(out=w_scales[i:P:32, :, :].bitcast(I32), in_=w4_rows[i].bitcast(I32))
+        load_w4_planes(nc.sync, head_planes, slice(0, HEAD))
         for a in range(1, PASSES):
             load_pass(a)
-        for q in range(4):
-            nc.gpsimd.dma_start(
-                out=w8_planes[32 * q + 4 : 32 * q + 4 + 4 * PASSES, :].bitcast(I32),
-                in_=w8_scales[:, 4 * q : 4 * q + 4, :].bitcast(I32),
-            )
+        load_w8_planes(nc.gpsimd)
+        load_w4_planes(nc.gpsimd, rest_planes, slice(HEAD, M))
         load_w8(0)
         load_r(0)
         load_w8(1)
-        for c in range(1, len(R_EDGES) - 1):
-            load_r(c)
+        load_r(1)
+        load_w8(2)
+        load_r(2)
+        nc.sync.dma_start(out=w4_rest[:].bitcast(I32), in_=w4_hbm[:, :, 2 * HEAD :].bitcast(I32))
+        load_r(3)
+        load_r(4)
 
         x_codes = [keep.tile([P, T], U32, name="x_codes_%d" % a, align_bytes=64) for a in range(PASSES)]
         x_scales = [keep.tile([P, T], U8, name="x_scales_%d" % a, align_bytes=64) for a in range(PASSES)]
 
         def quantize_pass(a):
             grouped = keep.tile([P, T, PACK], BF16, name="grouped_%d" % a, align_bytes=64)
-            dst = grouped[:].rearrange("p (c i) j -> p c j i", i=4)
-            src = raw[a][:].rearrange("p j (c i) -> p c j i", i=4)
-            nc.vector.tensor_copy(out=dst[:, : T // 8], in_=src[:, : T // 8])
-            nc.vector.tensor_copy(out=dst[:, T // 8 : DVE_COLS // 4], in_=src[:, T // 8 : DVE_COLS // 4])
-            nc.scalar.copy(out=dst[:, DVE_COLS // 4 :], in_=src[:, DVE_COLS // 4 :])
-            for cols in halves:
+
+            def quantize(cols):
                 nc.vector.quantize_mx(
                     out=x_codes[a][:, cols].bitcast(FP8X4),
                     scales=x_scales[a][:, cols],
                     in_=grouped[:, cols, :].rearrange("p t j -> p (t j)"),
                 )
+
+            for cols in x_parts[a]:
+                dst = grouped[:, cols, :].rearrange("p (c i) j -> p c j i", i=4)
+                src = raw[a, cols.start][:].rearrange("p j (c i) -> p c j i", i=4)
+                cut = (cols.stop - cols.start) * DVE_COLS // T // 4
+                first = min(cut, T // 2 // 4)
+                nc.vector.tensor_copy(out=dst[:, :first], in_=src[:, :first])
+                if first < cut:
+                    nc.vector.tensor_copy(out=dst[:, first:cut], in_=src[:, first:cut])
+                nc.scalar.copy(out=dst[:, cut:], in_=src[:, cut:])
+                for half in halves:
+                    if cols.start <= half.start < cols.stop:
+                        quantize(half)
 
         g_acc = {}
         u_acc = {}
@@ -108,10 +142,16 @@ def tile_mix_glu48_fm_res_kernel(tc, x, w4_words, w4_scales, w8_words, w8_scales
         def gate_pass(n, a):
             if a == 0:
                 g_acc[n] = psum.tile([P, T], F32, name="acc", tag="acc")
+            if n < BANKS:
+                words = w4_head[a][:, 2 * n * P : 2 * (n + 1) * P]
+                plane = head_planes[:, a, n * P : (n + 1) * P]
+            else:
+                words = w4_rest[:, a, 2 * (n * P - HEAD) : 2 * ((n + 1) * P - HEAD)]
+                plane = rest_planes[:, a, n * P - HEAD : (n + 1) * P - HEAD]
             nc.tensor.matmul_mx(
                 out=g_acc[n][:],
-                lhsT=w4[a][:, 2 * n * P : 2 * (n + 1) * P].bitcast(FP4X4),
-                lhsT_scale=w_scales[:, a, n * P : (n + 1) * P],
+                lhsT=words.bitcast(FP4X4),
+                lhsT_scale=plane,
                 rhs=x_codes[a][:].bitcast(FP8X4),
                 rhs_scale=x_scales[a][:],
                 start=(a == 0),
@@ -123,7 +163,8 @@ def tile_mix_glu48_fm_res_kernel(tc, x, w4_words, w4_scales, w8_words, w8_scales
         def up_product(n, cols):
             acc = psum.tile([P, T], F32, name="acc", tag="acc")
             u_acc[n, cols.start] = acc
-            b, c0 = divmod(n * P, W8_BLOCK)
+            b = max(i for i, lo in enumerate(W8_EDGES) if lo <= n)
+            c0 = (n - W8_EDGES[b]) * P
             for a in range(PASSES):
                 nc.tensor.matmul_mx(
                     out=acc[:, cols],
@@ -148,12 +189,17 @@ def tile_mix_glu48_fm_res_kernel(tc, x, w4_words, w4_scales, w8_words, w8_scales
         def store(tiles, cols):
             nc.sync.dma_start(out=out_tiles[:, tiles, cols], in_=res[:, tiles, cols])
 
-        for a in range(PASSES):
+        for a in range(PASSES - 1):
             quantize_pass(a)
             for n in range(BANKS):
                 gate_pass(n, a)
+        quantize_pass(PASSES - 1)
         last = TILES - 1
+        for n in range(CLOSE_AHEAD):
+            gate_pass(n, PASSES - 1)
         for n in range(TILES):
+            if n + CLOSE_AHEAD < BANKS:
+                gate_pass(n + CLOSE_AHEAD, PASSES - 1)
             if n >= BANKS:
                 for a in range(PASSES):
                     gate_pass(n, a)
@@ -162,17 +208,16 @@ def tile_mix_glu48_fm_res_kernel(tc, x, w4_words, w4_scales, w8_words, w8_scales
                 up_product(n, cols)
             for cols in parts:
                 multiply(n, cols)
-            if n >= last - 1:
+            if n == last:
                 for cols in parts:
                     add(slice(n, n + 1), cols)
                     store(slice(n, n + 1), cols)
                 continue
-            if n == last - 2:
-                done = n + 1
-            elif n >= PAIR and n % PAIR == 0:
-                done = n
+            if n < BANKS - 1:
+                ready = range(max(n - 1, 0), n)
             else:
-                continue
-            add(slice(done - PAIR, done), whole)
-            if done in OUT_EDGES:
-                store(slice(OUT_EDGES[list(OUT_EDGES).index(done) - 1], done), whole)
+                ready = range(n - 1 if n < BANKS else n, n + 1)
+            for m in ready:
+                add(slice(m, m + 1), whole)
+                if m + 1 in STORE_FROM:
+                    store(slice(STORE_FROM[m + 1], m + 1), whole)

@@ -24,14 +24,16 @@ DVE_COLS = 320
 HEAD = BANKS * P
 W8_EDGES = (0, 2, 6, TILES)
 CLOSE_AHEAD = 3
+EARLY_TILES = 6
 STORE_FROM = {4: 0, 8: 4, 10: 8, 11: 10}
-R_EDGES = (0, 2, 4, 6, 8, TILES)
+R_EDGES = (0, 2, 4, 6, 8, 10, TILES)
 
 
 def tile_mix_glu48_fm_res_kernel(tc, x, w4_words, w4_scales, w8_words, w8_scales, r, out):
     nc = tc.nc
     whole = slice(0, T)
     halves = [slice(0, T // 2), slice(T // 2, T)]
+    last_parts = [halves[0], slice(T // 2, 3 * T // 4), slice(3 * T // 4, T)]
     with ExitStack() as ctx:
         keep = ctx.enter_context(tc.tile_pool(name="keep", bufs=1))
         psum = ctx.enter_context(tc.psum_pool(name="psum", bufs=BANKS))
@@ -56,7 +58,7 @@ def tile_mix_glu48_fm_res_kernel(tc, x, w4_words, w4_scales, w8_words, w8_scales
             keep.tile([P, PASSES, (hi - lo) * P], U32, name="w8_%d" % lo, align_bytes=64)
             for lo, hi in zip(W8_EDGES, W8_EDGES[1:])
         ]
-        x_parts = [[whole]] * (PASSES - 1) + [halves]
+        x_parts = [halves] * PASSES
         raw = {
             (a, cols.start): keep.tile([P, PACK, cols.stop - cols.start], F32, name="raw_%d_%d" % (a, cols.start))
             for a in range(PASSES)
@@ -72,7 +74,10 @@ def tile_mix_glu48_fm_res_kernel(tc, x, w4_words, w4_scales, w8_words, w8_scales
             rows = x[a * P * PACK : (a + 1) * P * PACK, :]
             for cols in x_parts[a]:
                 nc.sync.dma_start(out=raw[a, cols.start][:], in_=rows.rearrange("(p j) t -> p j t", j=PACK)[:, :, cols])
-            nc.sync.dma_start(out=w4_head[a][:].bitcast(I32), in_=w4_hbm[:, a, : 2 * HEAD].bitcast(I32))
+                if cols.start == (0 if a == 0 else T // 2):
+                    nc.sync.dma_start(out=w4_head[a][:].bitcast(I32), in_=w4_hbm[:, a, : 2 * HEAD].bitcast(I32))
+                    if a == 0:
+                        load_w4_planes(nc.sync, head_planes, slice(0, HEAD))
 
         def load_w8(b):
             cols = slice(4 * P * W8_EDGES[b], 4 * P * W8_EDGES[b + 1])
@@ -94,9 +99,7 @@ def tile_mix_glu48_fm_res_kernel(tc, x, w4_words, w4_scales, w8_words, w8_scales
                     in_=w8_scales[:, 4 * q : 4 * q + 4, :].bitcast(I32),
                 )
 
-        load_pass(0)
-        load_w4_planes(nc.sync, head_planes, slice(0, HEAD))
-        for a in range(1, PASSES):
+        for a in range(PASSES):
             load_pass(a)
         load_w8_planes(nc.gpsimd)
         load_w4_planes(nc.gpsimd, rest_planes, slice(HEAD, M))
@@ -109,6 +112,7 @@ def tile_mix_glu48_fm_res_kernel(tc, x, w4_words, w4_scales, w8_words, w8_scales
         nc.sync.dma_start(out=w4_rest[:].bitcast(I32), in_=w4_hbm[:, :, 2 * HEAD :].bitcast(I32))
         load_r(3)
         load_r(4)
+        load_r(5)
 
         x_codes = [keep.tile([P, T], U32, name="x_codes_%d" % a, align_bytes=64) for a in range(PASSES)]
         x_scales = [keep.tile([P, T], U8, name="x_scales_%d" % a, align_bytes=64) for a in range(PASSES)]
@@ -139,8 +143,8 @@ def tile_mix_glu48_fm_res_kernel(tc, x, w4_words, w4_scales, w8_words, w8_scales
         g_acc = {}
         u_acc = {}
 
-        def gate_pass(n, a):
-            if a == 0:
+        def gate_pass(n, a, cols=whole):
+            if a == 0 and cols.start == 0:
                 g_acc[n] = psum.tile([P, T], F32, name="acc", tag="acc")
             if n < BANKS:
                 words = w4_head[a][:, 2 * n * P : 2 * (n + 1) * P]
@@ -149,16 +153,17 @@ def tile_mix_glu48_fm_res_kernel(tc, x, w4_words, w4_scales, w8_words, w8_scales
                 words = w4_rest[:, a, 2 * (n * P - HEAD) : 2 * ((n + 1) * P - HEAD)]
                 plane = rest_planes[:, a, n * P - HEAD : (n + 1) * P - HEAD]
             nc.tensor.matmul_mx(
-                out=g_acc[n][:],
+                out=g_acc[n][:, cols],
                 lhsT=words.bitcast(FP4X4),
                 lhsT_scale=plane,
-                rhs=x_codes[a][:].bitcast(FP8X4),
-                rhs_scale=x_scales[a][:],
-                start=(a == 0),
+                rhs=x_codes[a][:, cols].bitcast(FP8X4),
+                rhs_scale=x_scales[a][:, cols],
+                start=(a == 0 and cols.start == 0),
                 stop=(a == PASSES - 1),
             )
             if a == PASSES - 1:
-                nc.scalar.activation(out=act[n][:], in_=g_acc[n][:], func=SILU)
+                for part in halves if n == TILES - 1 else [whole]:
+                    nc.scalar.activation(out=act[n][:, part], in_=g_acc[n][:, part], func=SILU)
 
         def up_product(n, cols):
             acc = psum.tile([P, T], F32, name="acc", tag="acc")
@@ -189,7 +194,17 @@ def tile_mix_glu48_fm_res_kernel(tc, x, w4_words, w4_scales, w8_words, w8_scales
         def store(tiles, cols):
             nc.sync.dma_start(out=out_tiles[:, tiles, cols], in_=res[:, tiles, cols])
 
-        for a in range(PASSES - 1):
+        quantize_pass(0)
+        quarters = [slice(q * P, (q + 1) * P) for q in range(T // P)]
+        for n in range(EARLY_TILES):
+            for cols in quarters[:2]:
+                gate_pass(n, 0, cols)
+        for n in range(EARLY_TILES, BANKS):
+            gate_pass(n, 0)
+        for n in range(EARLY_TILES):
+            for cols in quarters[2:]:
+                gate_pass(n, 0, cols)
+        for a in range(1, PASSES - 1):
             quantize_pass(a)
             for n in range(BANKS):
                 gate_pass(n, a)
@@ -203,13 +218,13 @@ def tile_mix_glu48_fm_res_kernel(tc, x, w4_words, w4_scales, w8_words, w8_scales
             if n >= BANKS:
                 for a in range(PASSES):
                     gate_pass(n, a)
-            parts = halves if n == last else [whole]
+            parts = last_parts if n == last else [whole]
             for cols in parts:
                 up_product(n, cols)
             for cols in parts:
                 multiply(n, cols)
             if n == last:
-                for cols in parts:
+                for cols in halves:
                     add(slice(n, n + 1), cols)
                     store(slice(n, n + 1), cols)
                 continue

@@ -20,13 +20,12 @@ PACK = 4
 PASSES = K // (P * PACK)
 TILES = M // P
 BANKS = 8
-DVE_COLS = 320
+DVE_COLS = 352
 HEAD = BANKS * P
-W8_EDGES = (0, 2, 6, TILES)
-CLOSE_AHEAD = 3
-EARLY_TILES = 6
+W8_EDGES = (0, 3, 7, TILES)
+CLOSE_AHEAD = 4
 STORE_FROM = {4: 0, 8: 4, 10: 8, 11: 10}
-R_EDGES = (0, 2, 4, 6, 8, 10, TILES)
+R_EDGES = (0, 3, 6, 9, TILES)
 
 
 def tile_mix_glu48_fm_res_kernel(tc, x, w4_words, w4_scales, w8_words, w8_scales, r, out):
@@ -39,26 +38,25 @@ def tile_mix_glu48_fm_res_kernel(tc, x, w4_words, w4_scales, w8_words, w8_scales
         psum = ctx.enter_context(tc.psum_pool(name="psum", bufs=BANKS))
         ctx.enter_context(tc.manual_schedule())
 
-        head_planes = keep.tile([P, PASSES, HEAD], U8, name="head_planes", align_bytes=64)
-        rest_planes = keep.tile([P, PASSES, M - HEAD], U8, name="rest_planes", align_bytes=64)
+        w4_planes = keep.tile([P, PASSES, M], U8, name="w4_planes", align_bytes=64)
         w8_planes = keep.tile([P, M], U8, name="w8_planes", align_bytes=64)
         warm_in = keep.tile([P, 8], F32, name="warm_in")
         warm_out = keep.tile([P, 8], F32, name="warm_out")
-        nc.vector.memset(head_planes[:].rearrange("p a n -> p (a n)").bitcast(I32), 0)
+        nc.vector.memset(w4_planes[:].rearrange("p a n -> p (a n)").bitcast(I32), 0)
         nc.vector.memset(warm_in[:], 0.0)
         nc.vector.memset(w8_planes[:].bitcast(I32), 0)
-        nc.vector.memset(rest_planes[:].rearrange("p a n -> p (a n)").bitcast(I32), 0)
         nc.scalar.activation(out=warm_out[:], in_=warm_in[:], func=SILU)
 
         w8_hbm = w8_words.rearrange("a p n t -> p a (n t)")
         w4_hbm = w4_words.rearrange("a p b -> p a b")
-        w4_head = [keep.tile([P, 2 * HEAD], U8, name="w4_head_%d" % a, align_bytes=64) for a in range(PASSES)]
+        w4_open = keep.tile([P, PASSES - 1, 2 * HEAD], U8, name="w4_open", align_bytes=64)
+        w4_close = keep.tile([P, 2 * HEAD], U8, name="w4_close", align_bytes=64)
         w4_rest = keep.tile([P, PASSES, 2 * (M - HEAD)], U8, name="w4_rest", align_bytes=64)
         w8 = [
             keep.tile([P, PASSES, (hi - lo) * P], U32, name="w8_%d" % lo, align_bytes=64)
             for lo, hi in zip(W8_EDGES, W8_EDGES[1:])
         ]
-        x_parts = [halves] * PASSES
+        x_parts = [[whole]] + [halves] * (PASSES - 1)
         raw = {
             (a, cols.start): keep.tile([P, PACK, cols.stop - cols.start], F32, name="raw_%d_%d" % (a, cols.start))
             for a in range(PASSES)
@@ -74,10 +72,6 @@ def tile_mix_glu48_fm_res_kernel(tc, x, w4_words, w4_scales, w8_words, w8_scales
             rows = x[a * P * PACK : (a + 1) * P * PACK, :]
             for cols in x_parts[a]:
                 nc.sync.dma_start(out=raw[a, cols.start][:], in_=rows.rearrange("(p j) t -> p j t", j=PACK)[:, :, cols])
-                if cols.start == (0 if a == 0 else T // 2):
-                    nc.sync.dma_start(out=w4_head[a][:].bitcast(I32), in_=w4_hbm[:, a, : 2 * HEAD].bitcast(I32))
-                    if a == 0:
-                        load_w4_planes(nc.sync, head_planes, slice(0, HEAD))
 
         def load_w8(b):
             cols = slice(4 * P * W8_EDGES[b], 4 * P * W8_EDGES[b + 1])
@@ -87,10 +81,10 @@ def tile_mix_glu48_fm_res_kernel(tc, x, w4_words, w4_scales, w8_words, w8_scales
             tiles = slice(R_EDGES[c], R_EDGES[c + 1])
             nc.sync.dma_start(out=res[:, tiles, :], in_=r_tiles[:, tiles, :])
 
-        def load_w4_planes(queue, planes, cols):
+        def load_w4_planes(queue):
             rows = w4_scales.rearrange("a (q i) n -> i q a n", i=4)
             for i in range(4):
-                queue.dma_start(out=planes[i:P:32, :, :].bitcast(I32), in_=rows[i][:, :, cols].bitcast(I32))
+                queue.dma_start(out=w4_planes[i:P:32, :, :].bitcast(I32), in_=rows[i].bitcast(I32))
 
         def load_w8_planes(queue):
             for q in range(4):
@@ -99,20 +93,21 @@ def tile_mix_glu48_fm_res_kernel(tc, x, w4_words, w4_scales, w8_words, w8_scales
                     in_=w8_scales[:, 4 * q : 4 * q + 4, :].bitcast(I32),
                 )
 
-        for a in range(PASSES):
-            load_pass(a)
+        load_w4_planes(nc.gpsimd)
         load_w8_planes(nc.gpsimd)
-        load_w4_planes(nc.gpsimd, rest_planes, slice(HEAD, M))
+        load_pass(0)
+        nc.sync.dma_start(out=w4_open[:].bitcast(I32), in_=w4_hbm[:, : PASSES - 1, : 2 * HEAD].bitcast(I32))
+        for a in range(1, PASSES):
+            load_pass(a)
+        nc.sync.dma_start(out=w4_close[:].bitcast(I32), in_=w4_hbm[:, PASSES - 1, : 2 * HEAD].bitcast(I32))
         load_w8(0)
         load_r(0)
         load_w8(1)
         load_r(1)
         load_w8(2)
-        load_r(2)
         nc.sync.dma_start(out=w4_rest[:].bitcast(I32), in_=w4_hbm[:, :, 2 * HEAD :].bitcast(I32))
+        load_r(2)
         load_r(3)
-        load_r(4)
-        load_r(5)
 
         x_codes = [keep.tile([P, T], U32, name="x_codes_%d" % a, align_bytes=64) for a in range(PASSES)]
         x_scales = [keep.tile([P, T], U8, name="x_scales_%d" % a, align_bytes=64) for a in range(PASSES)]
@@ -128,37 +123,35 @@ def tile_mix_glu48_fm_res_kernel(tc, x, w4_words, w4_scales, w8_words, w8_scales
                 )
 
             for cols in x_parts[a]:
-                dst = grouped[:, cols, :].rearrange("p (c i) j -> p c j i", i=4)
-                src = raw[a, cols.start][:].rearrange("p j (c i) -> p c j i", i=4)
-                cut = (cols.stop - cols.start) * DVE_COLS // T // 4
-                first = min(cut, T // 2 // 4)
-                nc.vector.tensor_copy(out=dst[:, :first], in_=src[:, :first])
-                if first < cut:
-                    nc.vector.tensor_copy(out=dst[:, first:cut], in_=src[:, first:cut])
-                nc.scalar.copy(out=dst[:, cut:], in_=src[:, cut:])
-                for half in halves:
-                    if cols.start <= half.start < cols.stop:
-                        quantize(half)
+                inside = [half for half in halves if cols.start <= half.start < cols.stop]
+                for half in inside:
+                    dst = grouped[:, half, :].rearrange("p (c i) j -> p c j i", i=4)
+                    src = raw[a, cols.start][:, :, half.start - cols.start : half.stop - cols.start]
+                    src = src.rearrange("p j (c i) -> p c j i", i=4)
+                    cut = DVE_COLS // 2 // 4
+                    nc.vector.tensor_copy(out=dst[:, :cut], in_=src[:, :cut])
+                    nc.scalar.copy(out=dst[:, cut:], in_=src[:, cut:])
+                for half in inside:
+                    quantize(half)
 
         g_acc = {}
         u_acc = {}
 
-        def gate_pass(n, a, cols=whole):
-            if a == 0 and cols.start == 0:
+        def gate_pass(n, a):
+            if a == 0:
                 g_acc[n] = psum.tile([P, T], F32, name="acc", tag="acc")
             if n < BANKS:
-                words = w4_head[a][:, 2 * n * P : 2 * (n + 1) * P]
-                plane = head_planes[:, a, n * P : (n + 1) * P]
+                row = w4_close if a == PASSES - 1 else w4_open[:, a]
+                words = row[:, 2 * n * P : 2 * (n + 1) * P]
             else:
                 words = w4_rest[:, a, 2 * (n * P - HEAD) : 2 * ((n + 1) * P - HEAD)]
-                plane = rest_planes[:, a, n * P - HEAD : (n + 1) * P - HEAD]
             nc.tensor.matmul_mx(
-                out=g_acc[n][:, cols],
+                out=g_acc[n][:],
                 lhsT=words.bitcast(FP4X4),
-                lhsT_scale=plane,
-                rhs=x_codes[a][:, cols].bitcast(FP8X4),
-                rhs_scale=x_scales[a][:, cols],
-                start=(a == 0 and cols.start == 0),
+                lhsT_scale=w4_planes[:, a, n * P : (n + 1) * P],
+                rhs=x_codes[a][:].bitcast(FP8X4),
+                rhs_scale=x_scales[a][:],
+                start=(a == 0),
                 stop=(a == PASSES - 1),
             )
             if a == PASSES - 1:
@@ -194,17 +187,7 @@ def tile_mix_glu48_fm_res_kernel(tc, x, w4_words, w4_scales, w8_words, w8_scales
         def store(tiles, cols):
             nc.sync.dma_start(out=out_tiles[:, tiles, cols], in_=res[:, tiles, cols])
 
-        quantize_pass(0)
-        quarters = [slice(q * P, (q + 1) * P) for q in range(T // P)]
-        for n in range(EARLY_TILES):
-            for cols in quarters[:2]:
-                gate_pass(n, 0, cols)
-        for n in range(EARLY_TILES, BANKS):
-            gate_pass(n, 0)
-        for n in range(EARLY_TILES):
-            for cols in quarters[2:]:
-                gate_pass(n, 0, cols)
-        for a in range(1, PASSES - 1):
+        for a in range(PASSES - 1):
             quantize_pass(a)
             for n in range(BANKS):
                 gate_pass(n, a)

@@ -24,6 +24,7 @@ DVE_COLS = 352
 HEAD = BANKS * P
 W8_EDGES = (0, 3, 7, TILES)
 CLOSE_AHEAD = 4
+CAUGHT_UP = 9
 STORE_FROM = {4: 0, 8: 4, 10: 8, 11: 10}
 R_EDGES = (0, 3, 6, 9, TILES)
 
@@ -32,19 +33,20 @@ def tile_mix_glu48_fm_res_kernel(tc, x, w4_words, w4_scales, w8_words, w8_scales
     nc = tc.nc
     whole = slice(0, T)
     halves = [slice(0, T // 2), slice(T // 2, T)]
-    last_parts = [halves[0], slice(T // 2, 3 * T // 4), slice(3 * T // 4, T)]
     with ExitStack() as ctx:
         keep = ctx.enter_context(tc.tile_pool(name="keep", bufs=1))
         psum = ctx.enter_context(tc.psum_pool(name="psum", bufs=BANKS))
         ctx.enter_context(tc.manual_schedule())
 
-        w4_planes = keep.tile([P, PASSES, M], U8, name="w4_planes", align_bytes=64)
+        head_planes = keep.tile([P, PASSES, HEAD], U8, name="head_planes", align_bytes=64)
+        rest_planes = keep.tile([P, PASSES, M - HEAD], U8, name="rest_planes", align_bytes=64)
         w8_planes = keep.tile([P, M], U8, name="w8_planes", align_bytes=64)
         warm_in = keep.tile([P, 8], F32, name="warm_in")
         warm_out = keep.tile([P, 8], F32, name="warm_out")
-        nc.vector.memset(w4_planes[:].rearrange("p a n -> p (a n)").bitcast(I32), 0)
+        nc.vector.memset(head_planes[:].rearrange("p a n -> p (a n)").bitcast(I32), 0)
         nc.vector.memset(warm_in[:], 0.0)
         nc.vector.memset(w8_planes[:].bitcast(I32), 0)
+        nc.vector.memset(rest_planes[:].rearrange("p a n -> p (a n)").bitcast(I32), 0)
         nc.scalar.activation(out=warm_out[:], in_=warm_in[:], func=SILU)
 
         w8_hbm = w8_words.rearrange("a p n t -> p a (n t)")
@@ -81,10 +83,10 @@ def tile_mix_glu48_fm_res_kernel(tc, x, w4_words, w4_scales, w8_words, w8_scales
             tiles = slice(R_EDGES[c], R_EDGES[c + 1])
             nc.sync.dma_start(out=res[:, tiles, :], in_=r_tiles[:, tiles, :])
 
-        def load_w4_planes(queue):
+        def load_w4_planes(queue, planes, cols):
             rows = w4_scales.rearrange("a (q i) n -> i q a n", i=4)
             for i in range(4):
-                queue.dma_start(out=w4_planes[i:P:32, :, :].bitcast(I32), in_=rows[i].bitcast(I32))
+                queue.dma_start(out=planes[i:P:32, :, :].bitcast(I32), in_=rows[i][:, :, cols].bitcast(I32))
 
         def load_w8_planes(queue):
             for q in range(4):
@@ -93,10 +95,11 @@ def tile_mix_glu48_fm_res_kernel(tc, x, w4_words, w4_scales, w8_words, w8_scales
                     in_=w8_scales[:, 4 * q : 4 * q + 4, :].bitcast(I32),
                 )
 
-        load_w4_planes(nc.gpsimd)
         load_w8_planes(nc.gpsimd)
+        load_w4_planes(nc.gpsimd, rest_planes, slice(HEAD, M))
         load_pass(0)
         nc.sync.dma_start(out=w4_open[:].bitcast(I32), in_=w4_hbm[:, : PASSES - 1, : 2 * HEAD].bitcast(I32))
+        load_w4_planes(nc.sync, head_planes, slice(0, HEAD))
         for a in range(1, PASSES):
             load_pass(a)
         nc.sync.dma_start(out=w4_close[:].bitcast(I32), in_=w4_hbm[:, PASSES - 1, : 2 * HEAD].bitcast(I32))
@@ -143,12 +146,14 @@ def tile_mix_glu48_fm_res_kernel(tc, x, w4_words, w4_scales, w8_words, w8_scales
             if n < BANKS:
                 row = w4_close if a == PASSES - 1 else w4_open[:, a]
                 words = row[:, 2 * n * P : 2 * (n + 1) * P]
+                plane = head_planes[:, a, n * P : (n + 1) * P]
             else:
                 words = w4_rest[:, a, 2 * (n * P - HEAD) : 2 * ((n + 1) * P - HEAD)]
+                plane = rest_planes[:, a, n * P - HEAD : (n + 1) * P - HEAD]
             nc.tensor.matmul_mx(
                 out=g_acc[n][:],
                 lhsT=words.bitcast(FP4X4),
-                lhsT_scale=w4_planes[:, a, n * P : (n + 1) * P],
+                lhsT_scale=plane,
                 rhs=x_codes[a][:].bitcast(FP8X4),
                 rhs_scale=x_scales[a][:],
                 start=(a == 0),
@@ -193,6 +198,7 @@ def tile_mix_glu48_fm_res_kernel(tc, x, w4_words, w4_scales, w8_words, w8_scales
                 gate_pass(n, a)
         quantize_pass(PASSES - 1)
         last = TILES - 1
+        added = 0
         for n in range(CLOSE_AHEAD):
             gate_pass(n, PASSES - 1)
         for n in range(TILES):
@@ -201,7 +207,7 @@ def tile_mix_glu48_fm_res_kernel(tc, x, w4_words, w4_scales, w8_words, w8_scales
             if n >= BANKS:
                 for a in range(PASSES):
                     gate_pass(n, a)
-            parts = last_parts if n == last else [whole]
+            parts = halves if n == last else [whole]
             for cols in parts:
                 up_product(n, cols)
             for cols in parts:
@@ -211,10 +217,8 @@ def tile_mix_glu48_fm_res_kernel(tc, x, w4_words, w4_scales, w8_words, w8_scales
                     add(slice(n, n + 1), cols)
                     store(slice(n, n + 1), cols)
                 continue
-            if n < BANKS - 1:
-                ready = range(max(n - 1, 0), n)
-            else:
-                ready = range(n - 1 if n < BANKS else n, n + 1)
+            ready = range(added, n if 0 < n < CAUGHT_UP else n + 1)
+            added = ready.stop
             for m in ready:
                 add(slice(m, m + 1), whole)
                 if m + 1 in STORE_FROM:

@@ -20,11 +20,12 @@ PACK = 4
 PASSES = K // (P * PACK)
 TILES = M // P
 BANKS = 8
-DVE_COLS = 352
+DVE_COLS = 320
 HEAD = BANKS * P
 W8_EDGES = (0, 3, 7, TILES)
 CLOSE_AHEAD = 4
 CAUGHT_UP = 9
+EARLY_TILES = 6
 STORE_FROM = {4: 0, 8: 4, 10: 8, 11: 10}
 R_EDGES = (0, 3, 6, 9, TILES)
 
@@ -51,14 +52,13 @@ def tile_mix_glu48_fm_res_kernel(tc, x, w4_words, w4_scales, w8_words, w8_scales
 
         w8_hbm = w8_words.rearrange("a p n t -> p a (n t)")
         w4_hbm = w4_words.rearrange("a p b -> p a b")
-        w4_open = keep.tile([P, PASSES - 1, 2 * HEAD], U8, name="w4_open", align_bytes=64)
-        w4_close = keep.tile([P, 2 * HEAD], U8, name="w4_close", align_bytes=64)
+        w4_head = [keep.tile([P, 2 * HEAD], U8, name="w4_head_%d" % a, align_bytes=64) for a in range(PASSES)]
         w4_rest = keep.tile([P, PASSES, 2 * (M - HEAD)], U8, name="w4_rest", align_bytes=64)
         w8 = [
             keep.tile([P, PASSES, (hi - lo) * P], U32, name="w8_%d" % lo, align_bytes=64)
             for lo, hi in zip(W8_EDGES, W8_EDGES[1:])
         ]
-        x_parts = [[whole]] + [halves] * (PASSES - 1)
+        x_parts = [halves] * PASSES
         raw = {
             (a, cols.start): keep.tile([P, PACK, cols.stop - cols.start], F32, name="raw_%d_%d" % (a, cols.start))
             for a in range(PASSES)
@@ -74,6 +74,10 @@ def tile_mix_glu48_fm_res_kernel(tc, x, w4_words, w4_scales, w8_words, w8_scales
             rows = x[a * P * PACK : (a + 1) * P * PACK, :]
             for cols in x_parts[a]:
                 nc.sync.dma_start(out=raw[a, cols.start][:], in_=rows.rearrange("(p j) t -> p j t", j=PACK)[:, :, cols])
+                if cols.start == (0 if a == 0 else T // 2):
+                    nc.sync.dma_start(out=w4_head[a][:].bitcast(I32), in_=w4_hbm[:, a, : 2 * HEAD].bitcast(I32))
+                    if a == 0:
+                        load_w4_planes(nc.sync, head_planes, slice(0, HEAD))
 
         def load_w8(b):
             cols = slice(4 * P * W8_EDGES[b], 4 * P * W8_EDGES[b + 1])
@@ -95,14 +99,10 @@ def tile_mix_glu48_fm_res_kernel(tc, x, w4_words, w4_scales, w8_words, w8_scales
                     in_=w8_scales[:, 4 * q : 4 * q + 4, :].bitcast(I32),
                 )
 
+        for a in range(PASSES):
+            load_pass(a)
         load_w8_planes(nc.gpsimd)
         load_w4_planes(nc.gpsimd, rest_planes, slice(HEAD, M))
-        load_pass(0)
-        nc.sync.dma_start(out=w4_open[:].bitcast(I32), in_=w4_hbm[:, : PASSES - 1, : 2 * HEAD].bitcast(I32))
-        load_w4_planes(nc.sync, head_planes, slice(0, HEAD))
-        for a in range(1, PASSES):
-            load_pass(a)
-        nc.sync.dma_start(out=w4_close[:].bitcast(I32), in_=w4_hbm[:, PASSES - 1, : 2 * HEAD].bitcast(I32))
         load_w8(0)
         load_r(0)
         load_w8(1)
@@ -126,37 +126,37 @@ def tile_mix_glu48_fm_res_kernel(tc, x, w4_words, w4_scales, w8_words, w8_scales
                 )
 
             for cols in x_parts[a]:
-                inside = [half for half in halves if cols.start <= half.start < cols.stop]
-                for half in inside:
-                    dst = grouped[:, half, :].rearrange("p (c i) j -> p c j i", i=4)
-                    src = raw[a, cols.start][:, :, half.start - cols.start : half.stop - cols.start]
-                    src = src.rearrange("p j (c i) -> p c j i", i=4)
-                    cut = DVE_COLS // 2 // 4
-                    nc.vector.tensor_copy(out=dst[:, :cut], in_=src[:, :cut])
-                    nc.scalar.copy(out=dst[:, cut:], in_=src[:, cut:])
-                for half in inside:
-                    quantize(half)
+                dst = grouped[:, cols, :].rearrange("p (c i) j -> p c j i", i=4)
+                src = raw[a, cols.start][:].rearrange("p j (c i) -> p c j i", i=4)
+                cut = (cols.stop - cols.start) * DVE_COLS // T // 4
+                first = min(cut, T // 2 // 4)
+                nc.vector.tensor_copy(out=dst[:, :first], in_=src[:, :first])
+                if first < cut:
+                    nc.vector.tensor_copy(out=dst[:, first:cut], in_=src[:, first:cut])
+                nc.scalar.copy(out=dst[:, cut:], in_=src[:, cut:])
+                for half in halves:
+                    if cols.start <= half.start < cols.stop:
+                        quantize(half)
 
         g_acc = {}
         u_acc = {}
 
-        def gate_pass(n, a):
-            if a == 0:
+        def gate_pass(n, a, cols=whole):
+            if a == 0 and cols.start == 0:
                 g_acc[n] = psum.tile([P, T], F32, name="acc", tag="acc")
             if n < BANKS:
-                row = w4_close if a == PASSES - 1 else w4_open[:, a]
-                words = row[:, 2 * n * P : 2 * (n + 1) * P]
+                words = w4_head[a][:, 2 * n * P : 2 * (n + 1) * P]
                 plane = head_planes[:, a, n * P : (n + 1) * P]
             else:
                 words = w4_rest[:, a, 2 * (n * P - HEAD) : 2 * ((n + 1) * P - HEAD)]
                 plane = rest_planes[:, a, n * P - HEAD : (n + 1) * P - HEAD]
             nc.tensor.matmul_mx(
-                out=g_acc[n][:],
+                out=g_acc[n][:, cols],
                 lhsT=words.bitcast(FP4X4),
                 lhsT_scale=plane,
-                rhs=x_codes[a][:].bitcast(FP8X4),
-                rhs_scale=x_scales[a][:],
-                start=(a == 0),
+                rhs=x_codes[a][:, cols].bitcast(FP8X4),
+                rhs_scale=x_scales[a][:, cols],
+                start=(a == 0 and cols.start == 0),
                 stop=(a == PASSES - 1),
             )
             if a == PASSES - 1:
@@ -192,7 +192,17 @@ def tile_mix_glu48_fm_res_kernel(tc, x, w4_words, w4_scales, w8_words, w8_scales
         def store(tiles, cols):
             nc.sync.dma_start(out=out_tiles[:, tiles, cols], in_=res[:, tiles, cols])
 
-        for a in range(PASSES - 1):
+        quantize_pass(0)
+        quarters = [slice(q * P, (q + 1) * P) for q in range(T // P)]
+        for n in range(EARLY_TILES):
+            for cols in quarters[:2]:
+                gate_pass(n, 0, cols)
+        for n in range(EARLY_TILES, BANKS):
+            gate_pass(n, 0)
+        for n in range(EARLY_TILES):
+            for cols in quarters[2:]:
+                gate_pass(n, 0, cols)
+        for a in range(1, PASSES - 1):
             quantize_pass(a)
             for n in range(BANKS):
                 gate_pass(n, a)

@@ -20,7 +20,8 @@ PACK = 4
 PASSES = K // (P * PACK)
 TILES = M // P
 BANKS = 8
-DVE_COLS = 320
+CUTS = (0, 160)
+FINAL_CUTS = (0, 128, 192)
 HEAD = BANKS * P
 W8_EDGES = (0, 3, 7, TILES)
 CLOSE_AHEAD = 4
@@ -75,9 +76,9 @@ def tile_mix_glu48_fm_res_kernel(tc, x, w4_words, w4_scales, w8_words, w8_scales
             for cols in x_parts[a]:
                 nc.sync.dma_start(out=raw[a, cols.start][:], in_=rows.rearrange("(p j) t -> p j t", j=PACK)[:, :, cols])
                 if cols.start == (0 if a == 0 else T // 2):
-                    nc.sync.dma_start(out=w4_head[a][:].bitcast(I32), in_=w4_hbm[:, a, : 2 * HEAD].bitcast(I32))
                     if a == 0:
                         load_w4_planes(nc.sync, head_planes, slice(0, HEAD))
+                    nc.sync.dma_start(out=w4_head[a][:].bitcast(I32), in_=w4_hbm[:, a, : 2 * HEAD].bitcast(I32))
 
         def load_w8(b):
             cols = slice(4 * P * W8_EDGES[b], 4 * P * W8_EDGES[b + 1])
@@ -128,15 +129,14 @@ def tile_mix_glu48_fm_res_kernel(tc, x, w4_words, w4_scales, w8_words, w8_scales
             for cols in x_parts[a]:
                 dst = grouped[:, cols, :].rearrange("p (c i) j -> p c j i", i=4)
                 src = raw[a, cols.start][:].rearrange("p j (c i) -> p c j i", i=4)
-                cut = (cols.stop - cols.start) * DVE_COLS // T // 4
-                first = min(cut, T // 2 // 4)
-                nc.vector.tensor_copy(out=dst[:, :first], in_=src[:, :first])
-                if first < cut:
-                    nc.vector.tensor_copy(out=dst[:, first:cut], in_=src[:, first:cut])
-                nc.scalar.copy(out=dst[:, cut:], in_=src[:, cut:])
-                for half in halves:
-                    if cols.start <= half.start < cols.stop:
-                        quantize(half)
+                final = a == PASSES - 1 and cols.stop == T
+                cuts = [c // 4 for c in (FINAL_CUTS if final else CUTS)]
+                for lo, hi in zip(cuts, cuts[1:]):
+                    nc.vector.tensor_copy(out=dst[:, lo:hi], in_=src[:, lo:hi])
+                nc.scalar.copy(out=dst[:, cuts[-1] :], in_=src[:, cuts[-1] :])
+                step = P if final else T // 2
+                for lo in range(cols.start, cols.stop, step):
+                    quantize(slice(lo, lo + step))
 
         g_acc = {}
         u_acc = {}

@@ -20,14 +20,15 @@ PACK = 4
 PASSES = K // (P * PACK)
 TILES = M // P
 BANKS = 8
+ALIGN = 256
 CUTS = (0, 160)
 FINAL_CUTS = (0, 128, 192)
 HEAD = BANKS * P
 W8_EDGES = (0, 3, 7, TILES)
 CLOSE_AHEAD = 4
 CAUGHT_UP = 9
-EARLY_TILES = 6
-STORE_FROM = {4: 0, 8: 4, 10: 8, 11: 10}
+EARLY_TILES = 5
+STORE_FROM = {5: 0, 8: 5, 10: 8, 11: 10}
 R_EDGES = (0, 3, 6, 9, TILES)
 
 
@@ -40,34 +41,34 @@ def tile_mix_glu48_fm_res_kernel(tc, x, w4_words, w4_scales, w8_words, w8_scales
         psum = ctx.enter_context(tc.psum_pool(name="psum", bufs=BANKS))
         ctx.enter_context(tc.manual_schedule())
 
-        head_planes = keep.tile([P, PASSES, HEAD], U8, name="head_planes", align_bytes=64)
-        rest_planes = keep.tile([P, PASSES, M - HEAD], U8, name="rest_planes", align_bytes=64)
-        w8_planes = keep.tile([P, M], U8, name="w8_planes", align_bytes=64)
+        w4_planes = keep.tile([P, PASSES, M], U8, name="w4_planes", align_bytes=ALIGN)
+        w8_planes = keep.tile([P, M], U8, name="w8_planes", align_bytes=ALIGN)
         warm_in = keep.tile([P, 8], F32, name="warm_in")
         warm_out = keep.tile([P, 8], F32, name="warm_out")
-        nc.vector.memset(head_planes[:].rearrange("p a n -> p (a n)").bitcast(I32), 0)
+        nc.vector.memset(w4_planes[:].rearrange("p a n -> p (a n)").bitcast(I32), 0)
         nc.vector.memset(warm_in[:], 0.0)
         nc.vector.memset(w8_planes[:].bitcast(I32), 0)
-        nc.vector.memset(rest_planes[:].rearrange("p a n -> p (a n)").bitcast(I32), 0)
         nc.scalar.activation(out=warm_out[:], in_=warm_in[:], func=SILU)
 
         w8_hbm = w8_words.rearrange("a p n t -> p a (n t)")
         w4_hbm = w4_words.rearrange("a p b -> p a b")
-        w4_head = [keep.tile([P, 2 * HEAD], U8, name="w4_head_%d" % a, align_bytes=64) for a in range(PASSES)]
-        w4_rest = keep.tile([P, PASSES, 2 * (M - HEAD)], U8, name="w4_rest", align_bytes=64)
+        w4_head = [keep.tile([P, 2 * HEAD], U8, name="w4_head_%d" % a, align_bytes=ALIGN) for a in range(PASSES)]
+        w4_rest = keep.tile([P, PASSES, 2 * (M - HEAD)], U8, name="w4_rest", align_bytes=ALIGN)
         w8 = [
-            keep.tile([P, PASSES, (hi - lo) * P], U32, name="w8_%d" % lo, align_bytes=64)
+            keep.tile([P, PASSES, (hi - lo) * P], U32, name="w8_%d" % lo, align_bytes=ALIGN)
             for lo, hi in zip(W8_EDGES, W8_EDGES[1:])
         ]
         x_parts = [halves] * PASSES
         raw = {
-            (a, cols.start): keep.tile([P, PACK, cols.stop - cols.start], F32, name="raw_%d_%d" % (a, cols.start))
+            (a, cols.start): keep.tile(
+                [P, PACK, cols.stop - cols.start], F32, name="raw_%d_%d" % (a, cols.start), align_bytes=ALIGN
+            )
             for a in range(PASSES)
             for cols in x_parts[a]
         }
-        res = keep.tile([P, TILES, T], F32, name="res")
-        gated = keep.tile([P, TILES, T], F32, name="gated")
-        act = [keep.tile([P, T], F32, name="act_%d" % n) for n in range(TILES)]
+        res = keep.tile([P, TILES, T], F32, name="res", align_bytes=ALIGN)
+        gated = keep.tile([P, TILES, T], F32, name="gated", align_bytes=ALIGN)
+        act = [keep.tile([P, T], F32, name="act_%d" % n, align_bytes=ALIGN) for n in range(TILES)]
         r_tiles = r.rearrange("(n p) t -> p n t", p=P)
         out_tiles = out.rearrange("(n p) t -> p n t", p=P)
 
@@ -77,7 +78,7 @@ def tile_mix_glu48_fm_res_kernel(tc, x, w4_words, w4_scales, w8_words, w8_scales
                 nc.sync.dma_start(out=raw[a, cols.start][:], in_=rows.rearrange("(p j) t -> p j t", j=PACK)[:, :, cols])
                 if cols.start == (0 if a == 0 else T // 2):
                     if a == 0:
-                        load_w4_planes(nc.sync, head_planes, slice(0, HEAD))
+                        load_w4_planes()
                     nc.sync.dma_start(out=w4_head[a][:].bitcast(I32), in_=w4_hbm[:, a, : 2 * HEAD].bitcast(I32))
 
         def load_w8(b):
@@ -88,10 +89,10 @@ def tile_mix_glu48_fm_res_kernel(tc, x, w4_words, w4_scales, w8_words, w8_scales
             tiles = slice(R_EDGES[c], R_EDGES[c + 1])
             nc.sync.dma_start(out=res[:, tiles, :], in_=r_tiles[:, tiles, :])
 
-        def load_w4_planes(queue, planes, cols):
+        def load_w4_planes():
             rows = w4_scales.rearrange("a (q i) n -> i q a n", i=4)
             for i in range(4):
-                queue.dma_start(out=planes[i:P:32, :, :].bitcast(I32), in_=rows[i][:, :, cols].bitcast(I32))
+                nc.sync.dma_start(out=w4_planes[i:P:32, :, :].bitcast(I32), in_=rows[i].bitcast(I32))
 
         def load_w8_planes(queue):
             for q in range(4):
@@ -103,7 +104,6 @@ def tile_mix_glu48_fm_res_kernel(tc, x, w4_words, w4_scales, w8_words, w8_scales
         for a in range(PASSES):
             load_pass(a)
         load_w8_planes(nc.gpsimd)
-        load_w4_planes(nc.gpsimd, rest_planes, slice(HEAD, M))
         load_w8(0)
         load_r(0)
         load_w8(1)
@@ -113,11 +113,11 @@ def tile_mix_glu48_fm_res_kernel(tc, x, w4_words, w4_scales, w8_words, w8_scales
         load_r(2)
         load_r(3)
 
-        x_codes = [keep.tile([P, T], U32, name="x_codes_%d" % a, align_bytes=64) for a in range(PASSES)]
-        x_scales = [keep.tile([P, T], U8, name="x_scales_%d" % a, align_bytes=64) for a in range(PASSES)]
+        x_codes = [keep.tile([P, T], U32, name="x_codes_%d" % a, align_bytes=ALIGN) for a in range(PASSES)]
+        x_scales = [keep.tile([P, T], U8, name="x_scales_%d" % a, align_bytes=ALIGN) for a in range(PASSES)]
 
         def quantize_pass(a):
-            grouped = keep.tile([P, T, PACK], BF16, name="grouped_%d" % a, align_bytes=64)
+            grouped = keep.tile([P, T, PACK], BF16, name="grouped_%d" % a, align_bytes=ALIGN)
 
             def quantize(cols):
                 nc.vector.quantize_mx(
@@ -146,14 +146,12 @@ def tile_mix_glu48_fm_res_kernel(tc, x, w4_words, w4_scales, w8_words, w8_scales
                 g_acc[n] = psum.tile([P, T], F32, name="acc", tag="acc")
             if n < BANKS:
                 words = w4_head[a][:, 2 * n * P : 2 * (n + 1) * P]
-                plane = head_planes[:, a, n * P : (n + 1) * P]
             else:
                 words = w4_rest[:, a, 2 * (n * P - HEAD) : 2 * ((n + 1) * P - HEAD)]
-                plane = rest_planes[:, a, n * P - HEAD : (n + 1) * P - HEAD]
             nc.tensor.matmul_mx(
                 out=g_acc[n][:, cols],
                 lhsT=words.bitcast(FP4X4),
-                lhsT_scale=plane,
+                lhsT_scale=w4_planes[:, a, n * P : (n + 1) * P],
                 rhs=x_codes[a][:, cols].bitcast(FP8X4),
                 rhs_scale=x_scales[a][:, cols],
                 start=(a == 0 and cols.start == 0),

@@ -21,136 +21,134 @@ PASSES = K // (P * PACK)
 TILES = M // P
 BANKS = 8
 ALIGN = 256
+HALF = T // 2
+W8_ROW = 4
 CUTS = (0, 160)
 FINAL_CUTS = (0, 128, 192)
-HEAD = BANKS * P
-W8_EDGES = (0, 3, 7, TILES)
-CLOSE_AHEAD = 4
-CAUGHT_UP = 9
 EARLY_TILES = 5
-STORE_FROM = {5: 0, 8: 5, 10: 8, 11: 10}
+CLOSE_FIRST = 6
+POOL_COLS = 256
+POOL_TILES = 0
+W8_EDGES = (0, 3, 7, TILES)
 R_EDGES = (0, 3, 6, 9, TILES)
+OUT_EDGES = (0, 5, 8, 10, 11)
 
 
 def tile_mix_glu48_fm_res_kernel(tc, x, w4_words, w4_scales, w8_words, w8_scales, r, out):
     nc = tc.nc
     whole = slice(0, T)
-    halves = [slice(0, T // 2), slice(T // 2, T)]
+    halves = [slice(0, HALF), slice(HALF, T)]
     with ExitStack() as ctx:
         keep = ctx.enter_context(tc.tile_pool(name="keep", bufs=1))
         psum = ctx.enter_context(tc.psum_pool(name="psum", bufs=BANKS))
         ctx.enter_context(tc.manual_schedule())
 
-        w4_planes = keep.tile([P, PASSES, M], U8, name="w4_planes", align_bytes=ALIGN)
-        w8_planes = keep.tile([P, M], U8, name="w8_planes", align_bytes=ALIGN)
-        warm_in = keep.tile([P, 8], F32, name="warm_in")
-        warm_out = keep.tile([P, 8], F32, name="warm_out")
-        nc.vector.memset(w4_planes[:].rearrange("p a n -> p (a n)").bitcast(I32), 0)
-        nc.vector.memset(warm_in[:], 0.0)
-        nc.vector.memset(w8_planes[:].bitcast(I32), 0)
-        nc.scalar.activation(out=warm_out[:], in_=warm_in[:], func=SILU)
+        def sbuf(shape, dtype, name):
+            return keep.tile(shape, dtype, name=name, align_bytes=ALIGN)
 
-        w8_hbm = w8_words.rearrange("a p n t -> p a (n t)")
-        w4_hbm = w4_words.rearrange("a p b -> p a b")
-        w4_head = [keep.tile([P, 2 * HEAD], U8, name="w4_head_%d" % a, align_bytes=ALIGN) for a in range(PASSES)]
-        w4_rest = keep.tile([P, PASSES, 2 * (M - HEAD)], U8, name="w4_rest", align_bytes=ALIGN)
-        w8 = [
-            keep.tile([P, PASSES, (hi - lo) * P], U32, name="w8_%d" % lo, align_bytes=ALIGN)
-            for lo, hi in zip(W8_EDGES, W8_EDGES[1:])
-        ]
-        x_parts = [halves] * PASSES
-        raw = {
-            (a, cols.start): keep.tile(
-                [P, PACK, cols.stop - cols.start], F32, name="raw_%d_%d" % (a, cols.start), align_bytes=ALIGN
-            )
-            for a in range(PASSES)
-            for cols in x_parts[a]
-        }
-        res = keep.tile([P, TILES, T], F32, name="res", align_bytes=ALIGN)
-        gated = keep.tile([P, TILES, T], F32, name="gated", align_bytes=ALIGN)
-        act = [keep.tile([P, T], F32, name="act_%d" % n, align_bytes=ALIGN) for n in range(TILES)]
+        w4_planes = sbuf([P, PASSES, M], U8, "w4_planes")
+        w8_planes = sbuf([P, M], U8, "w8_planes")
+        table_in = sbuf([P, 8], F32, "table_in")
+        table_out = sbuf([P, 8], F32, "table_out")
+        nc.vector.memset(w4_planes[:].rearrange("p a n -> p (a n)").bitcast(I32), 0)
+        nc.vector.memset(table_in[:], 0.0)
+        nc.vector.memset(w8_planes[:].bitcast(I32), 0)
+        nc.scalar.activation(out=table_out[:], in_=table_in[:], func=SILU)
+
+        res = sbuf([P, TILES, T], F32, "res")
+        gated = sbuf([P, TILES, T], F32, "gated")
         r_tiles = r.rearrange("(n p) t -> p n t", p=P)
         out_tiles = out.rearrange("(n p) t -> p n t", p=P)
+        w4_hbm = w4_words.rearrange("a p b -> p a b")
+        w8_hbm = w8_words.rearrange("a p n i -> p a (n i)")
+        raw = {}
+        w4 = {}
+        w8 = {}
 
-        def load_pass(a):
-            rows = x[a * P * PACK : (a + 1) * P * PACK, :]
-            for cols in x_parts[a]:
-                nc.sync.dma_start(out=raw[a, cols.start][:], in_=rows.rearrange("(p j) t -> p j t", j=PACK)[:, :, cols])
-                if cols.start == (0 if a == 0 else T // 2):
-                    if a == 0:
-                        load_w4_planes()
-                    nc.sync.dma_start(out=w4_head[a][:].bitcast(I32), in_=w4_hbm[:, a, : 2 * HEAD].bitcast(I32))
+        def load_x(a, h):
+            raw[a, h] = sbuf([P, PACK, HALF], F32, "raw_%d_%d" % (a, h))
+            rows = x[a * P * PACK : (a + 1) * P * PACK, :].rearrange("(p j) t -> p j t", j=PACK)
+            nc.sync.dma_start(out=raw[a, h][:], in_=rows[:, :, halves[h]])
+
+        def load_planes(planes, scales, first_row):
+            rows = scales.rearrange("a (q i) n -> i q a n", i=4)
+            for i in range(4):
+                nc.sync.dma_start(out=planes[first_row + i : P : 32, :, :].bitcast(I32), in_=rows[i].bitcast(I32))
+
+        def load_w4(passes, tiles):
+            block = sbuf([P, len(passes), 2 * P * len(tiles)], U8, "w4_%d_%d" % (passes.start, tiles.start))
+            source = w4_hbm[:, passes.start : passes.stop, 2 * P * tiles.start : 2 * P * tiles.stop]
+            nc.sync.dma_start(out=block[:].bitcast(I32), in_=source.bitcast(I32))
+            for i, a in enumerate(passes):
+                for j, n in enumerate(tiles):
+                    w4[n, a] = block[:, i, 2 * P * j : 2 * P * (j + 1)]
 
         def load_w8(b):
-            cols = slice(4 * P * W8_EDGES[b], 4 * P * W8_EDGES[b + 1])
-            nc.sync.dma_start(out=w8[b][:].bitcast(I32), in_=w8_hbm[:, :, cols].bitcast(I32))
+            tiles = range(W8_EDGES[b], W8_EDGES[b + 1])
+            block = sbuf([P, PASSES, P * len(tiles)], U32, "w8_%d" % b)
+            source = w8_hbm[:, :, 4 * P * tiles.start : 4 * P * tiles.stop]
+            nc.sync.dma_start(out=block[:].bitcast(I32), in_=source.bitcast(I32))
+            for j, n in enumerate(tiles):
+                for a in range(PASSES):
+                    w8[n, a] = block[:, a, P * j : P * (j + 1)]
 
         def load_r(c):
             tiles = slice(R_EDGES[c], R_EDGES[c + 1])
             nc.sync.dma_start(out=res[:, tiles, :], in_=r_tiles[:, tiles, :])
 
-        def load_w4_planes():
-            rows = w4_scales.rearrange("a (q i) n -> i q a n", i=4)
-            for i in range(4):
-                nc.sync.dma_start(out=w4_planes[i:P:32, :, :].bitcast(I32), in_=rows[i].bitcast(I32))
-
-        def load_w8_planes(queue):
-            for q in range(4):
-                queue.dma_start(
-                    out=w8_planes[32 * q + 4 : 32 * q + 4 + 4 * PASSES, :].bitcast(I32),
-                    in_=w8_scales[:, 4 * q : 4 * q + 4, :].bitcast(I32),
-                )
-
-        for a in range(PASSES):
-            load_pass(a)
-        load_w8_planes(nc.gpsimd)
+        head = range(BANKS)
+        load_x(0, 0)
+        load_planes(w4_planes, w4_scales, 0)
+        load_w4(range(0, 1), head)
+        load_x(0, 1)
+        for a in range(1, PASSES):
+            load_x(a, 0)
+            load_x(a, 1)
+            load_w4(range(a, a + 1), head)
+        for q in range(4):
+            nc.sync.dma_start(
+                out=w8_planes[32 * q + W8_ROW : 32 * q + W8_ROW * (PASSES + 1), :].bitcast(I32),
+                in_=w8_scales[:, 4 * q : 4 * q + 4, :].bitcast(I32),
+            )
         load_w8(0)
         load_r(0)
         load_w8(1)
         load_r(1)
         load_w8(2)
-        nc.sync.dma_start(out=w4_rest[:].bitcast(I32), in_=w4_hbm[:, :, 2 * HEAD :].bitcast(I32))
+        load_w4(range(PASSES), range(BANKS, TILES))
         load_r(2)
         load_r(3)
 
-        x_codes = [keep.tile([P, T], U32, name="x_codes_%d" % a, align_bytes=ALIGN) for a in range(PASSES)]
-        x_scales = [keep.tile([P, T], U8, name="x_scales_%d" % a, align_bytes=ALIGN) for a in range(PASSES)]
+        x_codes = [sbuf([P, T], U32, "x_codes_%d" % a) for a in range(PASSES)]
+        x_scales = [sbuf([P, T], U8, "x_scales_%d" % a) for a in range(PASSES)]
 
         def quantize_pass(a):
-            grouped = keep.tile([P, T, PACK], BF16, name="grouped_%d" % a, align_bytes=ALIGN)
-
-            def quantize(cols):
-                nc.vector.quantize_mx(
-                    out=x_codes[a][:, cols].bitcast(FP8X4),
-                    scales=x_scales[a][:, cols],
-                    in_=grouped[:, cols, :].rearrange("p t j -> p (t j)"),
-                )
-
-            for cols in x_parts[a]:
+            grouped = sbuf([P, T, PACK], BF16, "grouped_%d" % a)
+            for h, cols in enumerate(halves):
                 dst = grouped[:, cols, :].rearrange("p (c i) j -> p c j i", i=4)
-                src = raw[a, cols.start][:].rearrange("p j (c i) -> p c j i", i=4)
-                final = a == PASSES - 1 and cols.stop == T
+                src = raw[a, h][:].rearrange("p j (c i) -> p c j i", i=4)
+                final = a == PASSES - 1 and h == 1
                 cuts = [c // 4 for c in (FINAL_CUTS if final else CUTS)]
                 for lo, hi in zip(cuts, cuts[1:]):
                     nc.vector.tensor_copy(out=dst[:, lo:hi], in_=src[:, lo:hi])
                 nc.scalar.copy(out=dst[:, cuts[-1] :], in_=src[:, cuts[-1] :])
-                step = P if final else T // 2
+                step = P if final else HALF
                 for lo in range(cols.start, cols.stop, step):
-                    quantize(slice(lo, lo + step))
+                    nc.vector.quantize_mx(
+                        out=x_codes[a][:, lo : lo + step].bitcast(FP8X4),
+                        scales=x_scales[a][:, lo : lo + step],
+                        in_=grouped[:, lo : lo + step, :].rearrange("p t j -> p (t j)"),
+                    )
 
-        g_acc = {}
-        u_acc = {}
+        gate = {}
+        act = {}
 
         def gate_pass(n, a, cols=whole):
-            if a == 0 and cols.start == 0:
-                g_acc[n] = psum.tile([P, T], F32, name="acc", tag="acc")
-            if n < BANKS:
-                words = w4_head[a][:, 2 * n * P : 2 * (n + 1) * P]
-            else:
-                words = w4_rest[:, a, 2 * (n * P - HEAD) : 2 * ((n + 1) * P - HEAD)]
+            if n not in gate:
+                gate[n] = psum.tile([P, T], F32, name="acc", tag="acc")
             nc.tensor.matmul_mx(
-                out=g_acc[n][:, cols],
-                lhsT=words.bitcast(FP4X4),
+                out=gate[n][:, cols],
+                lhsT=w4[n, a].bitcast(FP4X4),
                 lhsT_scale=w4_planes[:, a, n * P : (n + 1) * P],
                 rhs=x_codes[a][:, cols].bitcast(FP8X4),
                 rhs_scale=x_scales[a][:, cols],
@@ -158,34 +156,29 @@ def tile_mix_glu48_fm_res_kernel(tc, x, w4_words, w4_scales, w8_words, w8_scales
                 stop=(a == PASSES - 1),
             )
             if a == PASSES - 1:
+                act[n] = sbuf([P, T], F32, "act_%d" % n)
                 for part in halves if n == TILES - 1 else [whole]:
-                    nc.scalar.activation(out=act[n][:, part], in_=g_acc[n][:, part], func=SILU)
+                    nc.scalar.activation(out=act[n][:, part], in_=gate[n][:, part], func=SILU)
 
         def up_product(n, cols):
             acc = psum.tile([P, T], F32, name="acc", tag="acc")
-            u_acc[n, cols.start] = acc
-            b = max(i for i, lo in enumerate(W8_EDGES) if lo <= n)
-            c0 = (n - W8_EDGES[b]) * P
             for a in range(PASSES):
                 nc.tensor.matmul_mx(
                     out=acc[:, cols],
-                    lhsT=w8[b][:, a, c0 : c0 + P].bitcast(FP8X4),
-                    lhsT_scale=w8_planes[4 + 4 * a : P, n * P : (n + 1) * P],
+                    lhsT=w8[n, a].bitcast(FP8X4),
+                    lhsT_scale=w8_planes[W8_ROW * (a + 1) : P, n * P : (n + 1) * P],
                     rhs=x_codes[a][:, cols].bitcast(FP8X4),
                     rhs_scale=x_scales[a][:, cols],
                     start=(a == 0),
                     stop=(a == PASSES - 1),
                 )
+            return acc
 
-        def multiply(n, cols):
-            nc.vector.tensor_tensor(
-                out=gated[:, n, cols], in0=u_acc[n, cols.start][:, cols], in1=act[n][:, cols], op=ALU.mult
-            )
+        def multiply(n, acc, cols):
+            nc.vector.tensor_tensor(out=gated[:, n, cols], in0=acc[:, cols], in1=act[n][:, cols], op=ALU.mult)
 
-        def add(tiles, cols):
-            nc.vector.tensor_tensor(
-                out=res[:, tiles, cols], in0=gated[:, tiles, cols], in1=res[:, tiles, cols], op=ALU.add
-            )
+        def add(engine, n, cols):
+            engine.tensor_tensor(out=res[:, n, cols], in0=gated[:, n, cols], in1=res[:, n, cols], op=ALU.add)
 
         def store(tiles, cols):
             nc.sync.dma_start(out=out_tiles[:, tiles, cols], in_=res[:, tiles, cols])
@@ -202,32 +195,36 @@ def tile_mix_glu48_fm_res_kernel(tc, x, w4_words, w4_scales, w8_words, w8_scales
                 gate_pass(n, 0, cols)
         for a in range(1, PASSES - 1):
             quantize_pass(a)
-            for n in range(BANKS):
+            for n in head:
                 gate_pass(n, a)
         quantize_pass(PASSES - 1)
-        last = TILES - 1
-        added = 0
-        for n in range(CLOSE_AHEAD):
+        for n in range(CLOSE_FIRST):
             gate_pass(n, PASSES - 1)
-        for n in range(TILES):
-            if n + CLOSE_AHEAD < BANKS:
-                gate_pass(n + CLOSE_AHEAD, PASSES - 1)
+
+        added = 0
+        for n in range(TILES - 1):
             if n >= BANKS:
                 for a in range(PASSES):
                     gate_pass(n, a)
-            parts = halves if n == last else [whole]
-            for cols in parts:
-                up_product(n, cols)
-            for cols in parts:
-                multiply(n, cols)
-            if n == last:
-                for cols in halves:
-                    add(slice(n, n + 1), cols)
-                    store(slice(n, n + 1), cols)
-                continue
-            ready = range(added, n if 0 < n < CAUGHT_UP else n + 1)
+            acc = up_product(n, whole)
+            if n + CLOSE_FIRST < BANKS:
+                gate_pass(n + CLOSE_FIRST, PASSES - 1)
+            multiply(n, acc, whole)
+            if n < POOL_TILES:
+                add(nc.gpsimd, n, slice(0, POOL_COLS))
+            ready = range(added, n if 0 < n < 9 else n + 1)
             added = ready.stop
             for m in ready:
-                add(slice(m, m + 1), whole)
-                if m + 1 in STORE_FROM:
-                    store(slice(STORE_FROM[m + 1], m + 1), whole)
+                add(nc.vector, m, slice(POOL_COLS, T) if m < POOL_TILES else whole)
+                if m + 1 in OUT_EDGES:
+                    store(slice(OUT_EDGES[OUT_EDGES.index(m + 1) - 1], m + 1), whole)
+
+        last = TILES - 1
+        for a in range(PASSES):
+            gate_pass(last, a)
+        sums = [up_product(last, cols) for cols in halves]
+        for acc, cols in zip(sums, halves):
+            multiply(last, acc, cols)
+        for cols in halves:
+            add(nc.vector, last, cols)
+            store(slice(last, TILES), cols)

@@ -25,8 +25,9 @@ HALF = T // 2
 W8_ROW = 4
 CUTS = (0, 160)
 FINAL_CUTS = (0, 128, 192)
-EARLY_TILES = 5
-CLOSE_FIRST = 6
+EARLY_TILES = 6
+CLOSE_FIRST = 5
+AHEAD_OF_X = 5
 POOL_COLS = 256
 POOL_TILES = 0
 W8_EDGES = (0, 3, 7, TILES)
@@ -75,6 +76,13 @@ def tile_mix_glu48_fm_res_kernel(tc, x, w4_words, w4_scales, w8_words, w8_scales
             for i in range(4):
                 nc.sync.dma_start(out=planes[first_row + i : P : 32, :, :].bitcast(I32), in_=rows[i].bitcast(I32))
 
+        def load_w8_planes():
+            for q in range(4):
+                nc.sync.dma_start(
+                    out=w8_planes[32 * q + W8_ROW : 32 * q + W8_ROW * (PASSES + 1), :].bitcast(I32),
+                    in_=w8_scales[:, 4 * q : 4 * q + 4, :].bitcast(I32),
+                )
+
         def load_w4(passes, tiles):
             block = sbuf([P, len(passes), 2 * P * len(tiles)], U8, "w4_%d_%d" % (passes.start, tiles.start))
             source = w4_hbm[:, passes.start : passes.stop, 2 * P * tiles.start : 2 * P * tiles.stop]
@@ -104,12 +112,10 @@ def tile_mix_glu48_fm_res_kernel(tc, x, w4_words, w4_scales, w8_words, w8_scales
         for a in range(1, PASSES):
             load_x(a, 0)
             load_x(a, 1)
-            load_w4(range(a, a + 1), head)
-        for q in range(4):
-            nc.sync.dma_start(
-                out=w8_planes[32 * q + W8_ROW : 32 * q + W8_ROW * (PASSES + 1), :].bitcast(I32),
-                in_=w8_scales[:, 4 * q : 4 * q + 4, :].bitcast(I32),
-            )
+            if a == PASSES - 1:
+                load_w4(range(a - 1, a), range(AHEAD_OF_X, BANKS))
+                load_w8_planes()
+            load_w4(range(a, a + 1), head if a == PASSES - 1 else range(AHEAD_OF_X))
         load_w8(0)
         load_r(0)
         load_w8(1)
@@ -209,22 +215,25 @@ def tile_mix_glu48_fm_res_kernel(tc, x, w4_words, w4_scales, w8_words, w8_scales
             acc = up_product(n, whole)
             if n + CLOSE_FIRST < BANKS:
                 gate_pass(n + CLOSE_FIRST, PASSES - 1)
-            multiply(n, acc, whole)
-            if n < POOL_TILES:
-                add(nc.gpsimd, n, slice(0, POOL_COLS))
+            parts = halves if n == TILES - 2 else [whole]
+            for cols in parts:
+                multiply(n, acc, cols)
             ready = range(added, n if 0 < n < 9 else n + 1)
             added = ready.stop
             for m in ready:
-                add(nc.vector, m, slice(POOL_COLS, T) if m < POOL_TILES else whole)
+                for cols in parts:
+                    add(nc.vector, m, cols)
                 if m + 1 in OUT_EDGES:
                     store(slice(OUT_EDGES[OUT_EDGES.index(m + 1) - 1], m + 1), whole)
 
         last = TILES - 1
         for a in range(PASSES):
             gate_pass(last, a)
-        sums = [up_product(last, cols) for cols in halves]
-        for acc, cols in zip(sums, halves):
+        parts = [halves[0]] + quarters[2:]
+        sums = [up_product(last, cols) for cols in parts]
+        for acc, cols in zip(sums, parts):
             multiply(last, acc, cols)
-        for cols in halves:
+        for cols in parts:
             add(nc.vector, last, cols)
-            store(slice(last, TILES), cols)
+            if cols.stop != 3 * P:
+                store(slice(last, TILES), halves[cols.start // HALF])

@@ -23,22 +23,21 @@ BANKS = 8
 ALIGN = 256
 HALF = T // 2
 W8_ROW = 4
-CUTS = (0, 160)
-FINAL_CUTS = (0, 128, 192)
-EARLY_TILES = 6
-CLOSE_FIRST = 5
-AHEAD_OF_X = 5
-POOL_COLS = 256
-POOL_TILES = 0
-W8_EDGES = (0, 3, 7, TILES)
-R_EDGES = (0, 3, 6, 9, TILES)
+VECTOR_CAST = 160
+W8_EDGES = (0, 4, 8, TILES)
+R_EDGES = (0, 2, 5, 8, TILES)
 OUT_EDGES = (0, 5, 8, 10, 11)
+LATE_GATES_AFTER = range(7, 11)
+ADDS_PER_TILE = 2
+CATCH_UP = 7
+POOL_TILES = 4
 
 
 def tile_mix_glu48_fm_res_kernel(tc, x, w4_words, w4_scales, w8_words, w8_scales, r, out):
     nc = tc.nc
     whole = slice(0, T)
     halves = [slice(0, HALF), slice(HALF, T)]
+    last_pass = PASSES - 1
     with ExitStack() as ctx:
         keep = ctx.enter_context(tc.tile_pool(name="keep", bufs=1))
         psum = ctx.enter_context(tc.psum_pool(name="psum", bufs=BANKS))
@@ -66,15 +65,18 @@ def tile_mix_glu48_fm_res_kernel(tc, x, w4_words, w4_scales, w8_words, w8_scales
         w4 = {}
         w8 = {}
 
-        def load_x(a, h):
-            raw[a, h] = sbuf([P, PACK, HALF], F32, "raw_%d_%d" % (a, h))
+        def load_x(a, cols):
+            block = sbuf([P, PACK, cols.stop - cols.start], F32, "raw_%d_%d" % (a, cols.start))
             rows = x[a * P * PACK : (a + 1) * P * PACK, :].rearrange("(p j) t -> p j t", j=PACK)
-            nc.sync.dma_start(out=raw[a, h][:], in_=rows[:, :, halves[h]])
+            nc.sync.dma_start(out=block[:], in_=rows[:, :, cols])
+            for h, half in enumerate(halves):
+                if cols.start <= half.start and half.stop <= cols.stop:
+                    raw[a, h] = block[:, :, half.start - cols.start : half.stop - cols.start]
 
-        def load_planes(planes, scales, first_row):
-            rows = scales.rearrange("a (q i) n -> i q a n", i=4)
+        def load_w4_planes():
+            rows = w4_scales.rearrange("a (q i) n -> i q a n", i=4)
             for i in range(4):
-                nc.sync.dma_start(out=planes[first_row + i : P : 32, :, :].bitcast(I32), in_=rows[i].bitcast(I32))
+                nc.sync.dma_start(out=w4_planes[i:P:32, :, :].bitcast(I32), in_=rows[i].bitcast(I32))
 
         def load_w8_planes():
             for q in range(4):
@@ -105,46 +107,46 @@ def tile_mix_glu48_fm_res_kernel(tc, x, w4_words, w4_scales, w8_words, w8_scales
             nc.sync.dma_start(out=res[:, tiles, :], in_=r_tiles[:, tiles, :])
 
         head = range(BANKS)
-        load_x(0, 0)
-        load_planes(w4_planes, w4_scales, 0)
+        load_x(0, halves[0])
+        load_w4_planes()
         load_w4(range(0, 1), head)
-        load_x(0, 1)
-        for a in range(1, PASSES):
-            load_x(a, 0)
-            load_x(a, 1)
-            if a == PASSES - 1:
-                load_w4(range(a - 1, a), range(AHEAD_OF_X, BANKS))
-                load_w8_planes()
-            load_w4(range(a, a + 1), head if a == PASSES - 1 else range(AHEAD_OF_X))
+        load_x(0, halves[1])
+        load_x(1, halves[0])
+        load_w4(range(1, PASSES), head)
+        load_x(1, halves[1])
+        load_x(2, halves[0])
+        load_x(2, halves[1])
+        load_w8_planes()
         load_w8(0)
         load_r(0)
         load_w8(1)
         load_r(1)
-        load_w8(2)
         load_w4(range(PASSES), range(BANKS, TILES))
+        load_w8(2)
         load_r(2)
         load_r(3)
 
         x_codes = [sbuf([P, T], U32, "x_codes_%d" % a) for a in range(PASSES)]
         x_scales = [sbuf([P, T], U8, "x_scales_%d" % a) for a in range(PASSES)]
+        grouped = [sbuf([P, T, PACK], BF16, "grouped_%d" % a) for a in range(PASSES)]
 
-        def quantize_pass(a):
-            grouped = sbuf([P, T, PACK], BF16, "grouped_%d" % a)
-            for h, cols in enumerate(halves):
-                dst = grouped[:, cols, :].rearrange("p (c i) j -> p c j i", i=4)
-                src = raw[a, h][:].rearrange("p j (c i) -> p c j i", i=4)
-                final = a == PASSES - 1 and h == 1
-                cuts = [c // 4 for c in (FINAL_CUTS if final else CUTS)]
-                for lo, hi in zip(cuts, cuts[1:]):
-                    nc.vector.tensor_copy(out=dst[:, lo:hi], in_=src[:, lo:hi])
-                nc.scalar.copy(out=dst[:, cuts[-1] :], in_=src[:, cuts[-1] :])
-                step = P if final else HALF
-                for lo in range(cols.start, cols.stop, step):
-                    nc.vector.quantize_mx(
-                        out=x_codes[a][:, lo : lo + step].bitcast(FP8X4),
-                        scales=x_scales[a][:, lo : lo + step],
-                        in_=grouped[:, lo : lo + step, :].rearrange("p t j -> p (t j)"),
-                    )
+        def cast(engine_copy, a, h, lo, hi):
+            dst = grouped[a][:, halves[h], :].rearrange("p (c i) j -> p c j i", i=4)
+            src = raw[a, h].rearrange("p j (c i) -> p c j i", i=4)
+            engine_copy(out=dst[:, lo // 4 : hi // 4], in_=src[:, lo // 4 : hi // 4])
+
+        def quantize(a, cols):
+            nc.vector.quantize_mx(
+                out=x_codes[a][:, cols].bitcast(FP8X4),
+                scales=x_scales[a][:, cols],
+                in_=grouped[a][:, cols, :].rearrange("p t j -> p (t j)"),
+            )
+
+        def prepare(a, h, vector_cols=VECTOR_CAST):
+            if vector_cols:
+                cast(nc.vector.tensor_copy, a, h, 0, vector_cols)
+            cast(nc.scalar.copy, a, h, vector_cols, HALF)
+            quantize(a, halves[h])
 
         gate = {}
         act = {}
@@ -152,6 +154,7 @@ def tile_mix_glu48_fm_res_kernel(tc, x, w4_words, w4_scales, w8_words, w8_scales
         def gate_pass(n, a, cols=whole):
             if n not in gate:
                 gate[n] = psum.tile([P, T], F32, name="acc", tag="acc")
+            closing = a == last_pass and cols.stop == T
             nc.tensor.matmul_mx(
                 out=gate[n][:, cols],
                 lhsT=w4[n, a].bitcast(FP4X4),
@@ -159,9 +162,9 @@ def tile_mix_glu48_fm_res_kernel(tc, x, w4_words, w4_scales, w8_words, w8_scales
                 rhs=x_codes[a][:, cols].bitcast(FP8X4),
                 rhs_scale=x_scales[a][:, cols],
                 start=(a == 0 and cols.start == 0),
-                stop=(a == PASSES - 1),
+                stop=closing,
             )
-            if a == PASSES - 1:
+            if closing:
                 act[n] = sbuf([P, T], F32, "act_%d" % n)
                 for part in halves if n == TILES - 1 else [whole]:
                     nc.scalar.activation(out=act[n][:, part], in_=gate[n][:, part], func=SILU)
@@ -176,64 +179,52 @@ def tile_mix_glu48_fm_res_kernel(tc, x, w4_words, w4_scales, w8_words, w8_scales
                     rhs=x_codes[a][:, cols].bitcast(FP8X4),
                     rhs_scale=x_scales[a][:, cols],
                     start=(a == 0),
-                    stop=(a == PASSES - 1),
+                    stop=(a == last_pass),
                 )
             return acc
 
         def multiply(n, acc, cols):
             nc.vector.tensor_tensor(out=gated[:, n, cols], in0=acc[:, cols], in1=act[n][:, cols], op=ALU.mult)
 
-        def add(engine, n, cols):
+        def add(n, cols):
+            engine = nc.gpsimd if n < POOL_TILES else nc.vector
             engine.tensor_tensor(out=res[:, n, cols], in0=gated[:, n, cols], in1=res[:, n, cols], op=ALU.add)
 
         def store(tiles, cols):
             nc.sync.dma_start(out=out_tiles[:, tiles, cols], in_=res[:, tiles, cols])
 
-        quantize_pass(0)
-        quarters = [slice(q * P, (q + 1) * P) for q in range(T // P)]
-        for n in range(EARLY_TILES):
-            for cols in quarters[:2]:
-                gate_pass(n, 0, cols)
-        for n in range(EARLY_TILES, BANKS):
-            gate_pass(n, 0)
-        for n in range(EARLY_TILES):
-            for cols in quarters[2:]:
-                gate_pass(n, 0, cols)
-        for a in range(1, PASSES - 1):
-            quantize_pass(a)
-            for n in head:
-                gate_pass(n, a)
-        quantize_pass(PASSES - 1)
-        for n in range(CLOSE_FIRST):
-            gate_pass(n, PASSES - 1)
+        for a in range(PASSES):
+            for h in range(2):
+                prepare(a, h)
+                for n in head:
+                    gate_pass(n, a, halves[h])
 
+        late = list(range(BANKS, TILES))
         added = 0
         for n in range(TILES - 1):
-            if n >= BANKS:
-                for a in range(PASSES):
-                    gate_pass(n, a)
             acc = up_product(n, whole)
-            if n + CLOSE_FIRST < BANKS:
-                gate_pass(n + CLOSE_FIRST, PASSES - 1)
+            if n in LATE_GATES_AFTER:
+                for a in range(PASSES):
+                    gate_pass(late[0], a)
+                late.remove(late[0])
             parts = halves if n == TILES - 2 else [whole]
             for cols in parts:
                 multiply(n, acc, cols)
-            ready = range(added, n if 0 < n < 9 else n + 1)
+            ready = range(added, min(n + 1, POOL_TILES + ADDS_PER_TILE * max(0, n + 1 - CATCH_UP)))
             added = ready.stop
             for m in ready:
                 for cols in parts:
-                    add(nc.vector, m, cols)
+                    add(m, cols)
                 if m + 1 in OUT_EDGES:
                     store(slice(OUT_EDGES[OUT_EDGES.index(m + 1) - 1], m + 1), whole)
 
         last = TILES - 1
-        for a in range(PASSES):
-            gate_pass(last, a)
-        parts = [halves[0]] + quarters[2:]
+        parts = [halves[0], slice(HALF, HALF + P), slice(HALF + P, T)]
         sums = [up_product(last, cols) for cols in parts]
         for acc, cols in zip(sums, parts):
             multiply(last, acc, cols)
-        for cols in parts:
-            add(nc.vector, last, cols)
-            if cols.stop != 3 * P:
-                store(slice(last, TILES), halves[cols.start // HALF])
+        add(last, parts[0])
+        store(slice(last, TILES), halves[0])
+        add(last, parts[1])
+        add(last, parts[2])
+        store(slice(last, TILES), halves[1])

@@ -25,8 +25,8 @@ HALF = T // 2
 W8_ROW = 4
 VECTOR_CAST = 160
 W8_EDGES = (0, 4, 8, TILES)
-R_EDGES = (0, 2, 5, 8, TILES)
-OUT_EDGES = (0, 5, 8, 10, 11)
+R_EDGES = (0, 3, 6, 9, TILES)
+OUT_EDGES = (0, 4, 8, 10, 11)
 LATE_GATES_AFTER = range(7, 11)
 ADDS_PER_TILE = 2
 CATCH_UP = 7
@@ -43,8 +43,8 @@ def tile_mix_glu48_fm_res_kernel(tc, x, w4_words, w4_scales, w8_words, w8_scales
         psum = ctx.enter_context(tc.psum_pool(name="psum", bufs=BANKS))
         ctx.enter_context(tc.manual_schedule())
 
-        def sbuf(shape, dtype, name):
-            return keep.tile(shape, dtype, name=name, align_bytes=ALIGN)
+        def sbuf(shape, dtype, name, tag=None):
+            return keep.tile(shape, dtype, name=name, tag=tag or name, align_bytes=ALIGN)
 
         w4_planes = sbuf([P, PASSES, M], U8, "w4_planes")
         w8_planes = sbuf([P, M], U8, "w8_planes")
@@ -65,8 +65,8 @@ def tile_mix_glu48_fm_res_kernel(tc, x, w4_words, w4_scales, w8_words, w8_scales
         w4 = {}
         w8 = {}
 
-        def load_x(a, cols):
-            block = sbuf([P, PACK, cols.stop - cols.start], F32, "raw_%d_%d" % (a, cols.start))
+        def load_x(a, cols, tag=None):
+            block = sbuf([P, PACK, cols.stop - cols.start], F32, "raw_%d_%d" % (a, cols.start), tag)
             rows = x[a * P * PACK : (a + 1) * P * PACK, :].rearrange("(p j) t -> p j t", j=PACK)
             nc.sync.dma_start(out=block[:], in_=rows[:, :, cols])
             for h, half in enumerate(halves):
@@ -93,9 +93,9 @@ def tile_mix_glu48_fm_res_kernel(tc, x, w4_words, w4_scales, w8_words, w8_scales
                 for j, n in enumerate(tiles):
                     w4[n, a] = block[:, i, 2 * P * j : 2 * P * (j + 1)]
 
-        def load_w8(b):
+        def load_w8(b, tag=None):
             tiles = range(W8_EDGES[b], W8_EDGES[b + 1])
-            block = sbuf([P, PASSES, P * len(tiles)], U32, "w8_%d" % b)
+            block = sbuf([P, PASSES, P * len(tiles)], U32, "w8_%d" % b, tag)
             source = w8_hbm[:, :, 4 * P * tiles.start : 4 * P * tiles.stop]
             nc.sync.dma_start(out=block[:].bitcast(I32), in_=source.bitcast(I32))
             for j, n in enumerate(tiles):
@@ -112,10 +112,11 @@ def tile_mix_glu48_fm_res_kernel(tc, x, w4_words, w4_scales, w8_words, w8_scales
         load_w4(range(0, 1), head)
         load_x(0, halves[1])
         load_x(1, halves[0])
-        load_w4(range(1, PASSES), head)
+        load_w4(range(1, 2), head)
         load_x(1, halves[1])
         load_x(2, halves[0])
         load_x(2, halves[1])
+        load_w4(range(2, 3), head)
         load_w8_planes()
         load_w8(0)
         load_r(0)

@@ -27,10 +27,8 @@ VECTOR_CAST = 160
 W8_EDGES = (0, 4, 8, TILES)
 R_EDGES = (0, 3, 6, 9, TILES)
 OUT_EDGES = (0, 4, 8, 10, 11)
-LATE_GATES_AFTER = range(7, 11)
-ADDS_PER_TILE = 2
-CATCH_UP = 7
 POOL_TILES = 4
+ADDS_PER_TILE = 2
 
 
 def tile_mix_glu48_fm_res_kernel(tc, x, w4_words, w4_scales, w8_words, w8_scales, r, out):
@@ -38,13 +36,15 @@ def tile_mix_glu48_fm_res_kernel(tc, x, w4_words, w4_scales, w8_words, w8_scales
     whole = slice(0, T)
     halves = [slice(0, HALF), slice(HALF, T)]
     last_pass = PASSES - 1
+    head = range(BANKS)
+    late = range(BANKS, TILES)
     with ExitStack() as ctx:
         keep = ctx.enter_context(tc.tile_pool(name="keep", bufs=1))
         psum = ctx.enter_context(tc.psum_pool(name="psum", bufs=BANKS))
         ctx.enter_context(tc.manual_schedule())
 
-        def sbuf(shape, dtype, name, tag=None):
-            return keep.tile(shape, dtype, name=name, tag=tag or name, align_bytes=ALIGN)
+        def sbuf(shape, dtype, name):
+            return keep.tile(shape, dtype, name=name, tag=name, align_bytes=ALIGN)
 
         w4_planes = sbuf([P, PASSES, M], U8, "w4_planes")
         w8_planes = sbuf([P, M], U8, "w8_planes")
@@ -57,21 +57,17 @@ def tile_mix_glu48_fm_res_kernel(tc, x, w4_words, w4_scales, w8_words, w8_scales
 
         res = sbuf([P, TILES, T], F32, "res")
         gated = sbuf([P, TILES, T], F32, "gated")
+        raw = [sbuf([P, PACK, T], F32, "raw_%d" % a) for a in range(PASSES)]
         r_tiles = r.rearrange("(n p) t -> p n t", p=P)
         out_tiles = out.rearrange("(n p) t -> p n t", p=P)
+        x_rows = x.rearrange("(a p j) t -> a p j t", p=P, j=PACK)
         w4_hbm = w4_words.rearrange("a p b -> p a b")
         w8_hbm = w8_words.rearrange("a p n i -> p a (n i)")
-        raw = {}
         w4 = {}
         w8 = {}
 
-        def load_x(a, cols, tag=None):
-            block = sbuf([P, PACK, cols.stop - cols.start], F32, "raw_%d_%d" % (a, cols.start), tag)
-            rows = x[a * P * PACK : (a + 1) * P * PACK, :].rearrange("(p j) t -> p j t", j=PACK)
-            nc.sync.dma_start(out=block[:], in_=rows[:, :, cols])
-            for h, half in enumerate(halves):
-                if cols.start <= half.start and half.stop <= cols.stop:
-                    raw[a, h] = block[:, :, half.start - cols.start : half.stop - cols.start]
+        def load_x(a):
+            nc.sync.dma_start(out=raw[a][:], in_=x_rows[a])
 
         def load_w4_planes():
             rows = w4_scales.rearrange("a (q i) n -> i q a n", i=4)
@@ -93,9 +89,9 @@ def tile_mix_glu48_fm_res_kernel(tc, x, w4_words, w4_scales, w8_words, w8_scales
                 for j, n in enumerate(tiles):
                     w4[n, a] = block[:, i, 2 * P * j : 2 * P * (j + 1)]
 
-        def load_w8(b, tag=None):
+        def load_w8(b):
             tiles = range(W8_EDGES[b], W8_EDGES[b + 1])
-            block = sbuf([P, PASSES, P * len(tiles)], U32, "w8_%d" % b, tag)
+            block = sbuf([P, PASSES, P * len(tiles)], U32, "w8_%d" % b)
             source = w8_hbm[:, :, 4 * P * tiles.start : 4 * P * tiles.stop]
             nc.sync.dma_start(out=block[:].bitcast(I32), in_=source.bitcast(I32))
             for j, n in enumerate(tiles):
@@ -106,23 +102,19 @@ def tile_mix_glu48_fm_res_kernel(tc, x, w4_words, w4_scales, w8_words, w8_scales
             tiles = slice(R_EDGES[c], R_EDGES[c + 1])
             nc.sync.dma_start(out=res[:, tiles, :], in_=r_tiles[:, tiles, :])
 
-        head = range(BANKS)
-        load_x(0, halves[0])
+        load_x(0)
         load_w4_planes()
         load_w4(range(0, 1), head)
-        load_x(0, halves[1])
-        load_x(1, halves[0])
+        load_x(1)
         load_w4(range(1, 2), head)
-        load_x(1, halves[1])
-        load_x(2, halves[0])
-        load_x(2, halves[1])
+        load_x(2)
         load_w4(range(2, 3), head)
         load_w8_planes()
         load_w8(0)
         load_r(0)
         load_w8(1)
         load_r(1)
-        load_w4(range(PASSES), range(BANKS, TILES))
+        load_w4(range(PASSES), late)
         load_w8(2)
         load_r(2)
         load_r(3)
@@ -131,10 +123,10 @@ def tile_mix_glu48_fm_res_kernel(tc, x, w4_words, w4_scales, w8_words, w8_scales
         x_scales = [sbuf([P, T], U8, "x_scales_%d" % a) for a in range(PASSES)]
         grouped = [sbuf([P, T, PACK], BF16, "grouped_%d" % a) for a in range(PASSES)]
 
-        def cast(engine_copy, a, h, lo, hi):
-            dst = grouped[a][:, halves[h], :].rearrange("p (c i) j -> p c j i", i=4)
-            src = raw[a, h].rearrange("p j (c i) -> p c j i", i=4)
-            engine_copy(out=dst[:, lo // 4 : hi // 4], in_=src[:, lo // 4 : hi // 4])
+        def cast(engine_copy, a, cols):
+            dst = grouped[a][:, cols, :].rearrange("p (c i) j -> p c j i", i=4)
+            src = raw[a][:, :, cols].rearrange("p j (c i) -> p c j i", i=4)
+            engine_copy(out=dst, in_=src)
 
         def quantize(a, cols):
             nc.vector.quantize_mx(
@@ -143,16 +135,10 @@ def tile_mix_glu48_fm_res_kernel(tc, x, w4_words, w4_scales, w8_words, w8_scales
                 in_=grouped[a][:, cols, :].rearrange("p t j -> p (t j)"),
             )
 
-        def prepare(a, h, vector_cols=VECTOR_CAST):
-            if vector_cols:
-                cast(nc.vector.tensor_copy, a, h, 0, vector_cols)
-            cast(nc.scalar.copy, a, h, vector_cols, HALF)
-            quantize(a, halves[h])
-
         gate = {}
         act = {}
 
-        def gate_pass(n, a, cols=whole):
+        def gate_pass(n, a, cols):
             if n not in gate:
                 gate[n] = psum.tile([P, T], F32, name="acc", tag="acc")
             closing = a == last_pass and cols.stop == T
@@ -195,23 +181,24 @@ def tile_mix_glu48_fm_res_kernel(tc, x, w4_words, w4_scales, w8_words, w8_scales
             nc.sync.dma_start(out=out_tiles[:, tiles, cols], in_=res[:, tiles, cols])
 
         for a in range(PASSES):
-            for h in range(2):
-                prepare(a, h)
+            for half in halves:
+                split = half.start + VECTOR_CAST
+                cast(nc.vector.tensor_copy, a, slice(half.start, split))
+                cast(nc.scalar.copy, a, slice(split, half.stop))
+                quantize(a, half)
                 for n in head:
-                    gate_pass(n, a, halves[h])
+                    gate_pass(n, a, half)
 
-        late = list(range(BANKS, TILES))
         added = 0
         for n in range(TILES - 1):
             acc = up_product(n, whole)
-            if n in LATE_GATES_AFTER:
+            if n + 1 in late:
                 for a in range(PASSES):
-                    gate_pass(late[0], a)
-                late.remove(late[0])
+                    gate_pass(n + 1, a, whole)
             parts = halves if n == TILES - 2 else [whole]
             for cols in parts:
                 multiply(n, acc, cols)
-            ready = range(added, min(n + 1, POOL_TILES + ADDS_PER_TILE * max(0, n + 1 - CATCH_UP)))
+            ready = range(added, min(n + 1, POOL_TILES + ADDS_PER_TILE * max(0, n + 2 - BANKS)))
             added = ready.stop
             for m in ready:
                 for cols in parts:

@@ -47,12 +47,13 @@ def tile_mix_glu48_fm_res_kernel(tc, x, w4_words, w4_scales, w8_words, w8_scales
             return keep.tile(shape, dtype, name=name, tag=name, align_bytes=ALIGN)
 
         w4_planes = sbuf([P, PASSES, M], U8, "w4_planes")
-        w8_planes = sbuf([P, M], U8, "w8_planes")
+        w8_rows = sbuf([P, 2, M], U8, "w8_rows")
+        w8_planes = w8_rows[:, 0, :]
         table_in = sbuf([P, 8], F32, "table_in")
         table_out = sbuf([P, 8], F32, "table_out")
         nc.vector.memset(w4_planes[:].rearrange("p a n -> p (a n)").bitcast(I32), 0)
         nc.vector.memset(table_in[:], 0.0)
-        nc.vector.memset(w8_planes[:].bitcast(I32), 0)
+        nc.vector.memset(w8_rows[0:64].rearrange("p s n -> p (s n)").bitcast(I32), 0)
         nc.scalar.activation(out=table_out[:], in_=table_in[:], func=SILU)
 
         res = sbuf([P, TILES, T], F32, "res")
@@ -77,7 +78,7 @@ def tile_mix_glu48_fm_res_kernel(tc, x, w4_words, w4_scales, w8_words, w8_scales
         def load_w8_planes():
             for q in range(4):
                 nc.sync.dma_start(
-                    out=w8_planes[32 * q + W8_ROW : 32 * q + W8_ROW * (PASSES + 1), :].bitcast(I32),
+                    out=w8_rows[32 * (q % 2) : 32 * (q % 2) + W8_ROW * PASSES, q // 2, :].bitcast(I32),
                     in_=w8_scales[:, 4 * q : 4 * q + 4, :].bitcast(I32),
                 )
 
@@ -162,7 +163,7 @@ def tile_mix_glu48_fm_res_kernel(tc, x, w4_words, w4_scales, w8_words, w8_scales
                 nc.tensor.matmul_mx(
                     out=acc[:, cols],
                     lhsT=w8[n, a].bitcast(FP8X4),
-                    lhsT_scale=w8_planes[W8_ROW * (a + 1) : P, n * P : (n + 1) * P],
+                    lhsT_scale=w8_planes[W8_ROW * a : P, n * P : (n + 1) * P],
                     rhs=x_codes[a][:, cols].bitcast(FP8X4),
                     rhs_scale=x_scales[a][:, cols],
                     start=(a == 0),
@@ -188,6 +189,8 @@ def tile_mix_glu48_fm_res_kernel(tc, x, w4_words, w4_scales, w8_words, w8_scales
                 quantize(a, half)
                 for n in head:
                     gate_pass(n, a, half)
+
+        nc.vector.tensor_copy(out=w8_rows[64:P, 0, :].bitcast(I32), in_=w8_rows[0:64, 1, :].bitcast(I32))
 
         added = 0
         for n in range(TILES - 1):

@@ -58,7 +58,7 @@ def tile_mix_glu48_fm_res_kernel(tc, x, w4_words, w4_scales, w8_words, w8_scales
 
         res = sbuf([P, TILES, T], F32, "res")
         gated = sbuf([P, TILES, T], F32, "gated")
-        raw = [sbuf([P, PACK, T], F32, "raw_%d" % a) for a in range(PASSES)]
+        raw = {}
         r_tiles = r.rearrange("(n p) t -> p n t", p=P)
         out_tiles = out.rearrange("(n p) t -> p n t", p=P)
         x_rows = x.rearrange("(a p j) t -> a p j t", p=P, j=PACK)
@@ -67,8 +67,12 @@ def tile_mix_glu48_fm_res_kernel(tc, x, w4_words, w4_scales, w8_words, w8_scales
         w4 = {}
         w8 = {}
 
-        def load_x(a):
-            nc.sync.dma_start(out=raw[a][:], in_=x_rows[a])
+        def load_x(a, cols):
+            block = sbuf([P, PACK, cols.stop - cols.start], F32, "raw_%d_%d" % (a, cols.start))
+            nc.sync.dma_start(out=block[:], in_=x_rows[a][:, :, cols])
+            for half in halves:
+                if cols.start <= half.start < cols.stop:
+                    raw[a, half.start] = block[:, :, half.start - cols.start : half.stop - cols.start]
 
         def load_w4_planes():
             rows = w4_scales.rearrange("a (q i) n -> i q a n", i=4)
@@ -103,12 +107,14 @@ def tile_mix_glu48_fm_res_kernel(tc, x, w4_words, w4_scales, w8_words, w8_scales
             tiles = slice(R_EDGES[c], R_EDGES[c + 1])
             nc.sync.dma_start(out=res[:, tiles, :], in_=r_tiles[:, tiles, :])
 
-        load_x(0)
-        load_w4_planes()
+        load_x(0, halves[0])
         load_w4(range(0, 1), head)
-        load_x(1)
+        load_w4_planes()
+        load_x(0, halves[1])
+        load_x(1, whole)
         load_w4(range(1, 2), head)
-        load_x(2)
+        load_x(2, halves[0])
+        load_x(2, halves[1])
         load_w4(range(2, 3), head)
         load_w8_planes()
         load_w8(0)
@@ -124,9 +130,9 @@ def tile_mix_glu48_fm_res_kernel(tc, x, w4_words, w4_scales, w8_words, w8_scales
         x_scales = [sbuf([P, T], U8, "x_scales_%d" % a) for a in range(PASSES)]
         grouped = [sbuf([P, T, PACK], BF16, "grouped_%d" % a) for a in range(PASSES)]
 
-        def cast(engine_copy, a, cols):
-            dst = grouped[a][:, cols, :].rearrange("p (c i) j -> p c j i", i=4)
-            src = raw[a][:, :, cols].rearrange("p j (c i) -> p c j i", i=4)
+        def cast(engine_copy, a, half, share):
+            dst = grouped[a][:, half, :][:, share, :].rearrange("p (c i) j -> p c j i", i=4)
+            src = raw[a, half.start][:, :, share].rearrange("p j (c i) -> p c j i", i=4)
             engine_copy(out=dst, in_=src)
 
         def quantize(a, cols):
@@ -183,9 +189,8 @@ def tile_mix_glu48_fm_res_kernel(tc, x, w4_words, w4_scales, w8_words, w8_scales
 
         for a in range(PASSES):
             for half in halves:
-                split = half.start + VECTOR_CAST
-                cast(nc.vector.tensor_copy, a, slice(half.start, split))
-                cast(nc.scalar.copy, a, slice(split, half.stop))
+                cast(nc.vector.tensor_copy, a, half, slice(0, VECTOR_CAST))
+                cast(nc.scalar.copy, a, half, slice(VECTOR_CAST, HALF))
                 quantize(a, half)
                 for n in head:
                     gate_pass(n, a, half)

@@ -24,9 +24,9 @@ ALIGN = 256
 HALF = T // 2
 W8_ROW = 4
 VECTOR_CAST = 160
-W8_EDGES = (0, 4, 8, TILES)
+W8_EDGES = (0, 4, 8, 10, TILES)
 R_EDGES = (0, 3, 6, 9, TILES)
-OUT_EDGES = (0, 4, 8, 10, 11)
+OUT_EDGES = (0, 4, 6, 8, 10, 11)
 POOL_TILES = 4
 ADDS_PER_TILE = 2
 
@@ -124,6 +124,7 @@ def tile_mix_glu48_fm_res_kernel(tc, x, w4_words, w4_scales, w8_words, w8_scales
         load_w4(range(PASSES), late)
         load_w8(2)
         load_r(2)
+        load_w8(3)
         load_r(3)
 
         x_codes = [sbuf([P, T], U32, "x_codes_%d" % a) for a in range(PASSES)]

@@ -24,11 +24,11 @@ ALIGN = 256
 HALF = T // 2
 W8_ROW = 4
 VECTOR_CAST = 160
-W8_EDGES = (0, 4, 8, 10, TILES)
+W8_EDGES = (0, 2, 5, 8, 10, TILES)
 R_EDGES = (0, 3, 6, 9, TILES)
 OUT_EDGES = (0, 4, 6, 8, 10, 11)
-POOL_TILES = 4
-ADDS_PER_TILE = 2
+POOL_TILES = (0, 1, 2, 3)
+ADDED_AFTER = {0: 1, 1: 2, 2: 3, 3: 4, 7: 6, 8: 8, 9: 10}
 
 
 def tile_mix_glu48_fm_res_kernel(tc, x, w4_words, w4_scales, w8_words, w8_scales, r, out):
@@ -57,7 +57,7 @@ def tile_mix_glu48_fm_res_kernel(tc, x, w4_words, w4_scales, w8_words, w8_scales
         nc.scalar.activation(out=table_out[:], in_=table_in[:], func=SILU)
 
         res = sbuf([P, TILES, T], F32, "res")
-        gated = sbuf([P, TILES, T], F32, "gated")
+        slots = sbuf([P, TILES + 1, T], F32, "slots")
         raw = {}
         r_tiles = r.rearrange("(n p) t -> p n t", p=P)
         out_tiles = out.rearrange("(n p) t -> p n t", p=P)
@@ -112,19 +112,19 @@ def tile_mix_glu48_fm_res_kernel(tc, x, w4_words, w4_scales, w8_words, w8_scales
         load_w4_planes()
         load_x(0, halves[1])
         load_x(1, whole)
-        load_w4(range(1, 2), head)
+        load_w4(range(1, 3), head)
         load_x(2, halves[0])
         load_x(2, halves[1])
-        load_w4(range(2, 3), head)
         load_w8_planes()
         load_w8(0)
-        load_r(0)
         load_w8(1)
+        load_r(0)
+        load_w8(2)
         load_r(1)
         load_w4(range(PASSES), late)
-        load_w8(2)
-        load_r(2)
         load_w8(3)
+        load_r(2)
+        load_w8(4)
         load_r(3)
 
         x_codes = [sbuf([P, T], U32, "x_codes_%d" % a) for a in range(PASSES)]
@@ -179,11 +179,11 @@ def tile_mix_glu48_fm_res_kernel(tc, x, w4_words, w4_scales, w8_words, w8_scales
             return acc
 
         def multiply(n, acc, cols):
-            nc.vector.tensor_tensor(out=gated[:, n, cols], in0=acc[:, cols], in1=act[n][:, cols], op=ALU.mult)
+            nc.vector.tensor_tensor(out=slots[:, n + 1, cols], in0=acc[:, cols], in1=act[n][:, cols], op=ALU.mult)
 
         def add(n, cols):
-            engine = nc.gpsimd if n < POOL_TILES else nc.vector
-            engine.tensor_tensor(out=res[:, n, cols], in0=gated[:, n, cols], in1=res[:, n, cols], op=ALU.add)
+            engine = nc.gpsimd if n in POOL_TILES else nc.vector
+            engine.tensor_tensor(out=res[:, n, cols], in0=slots[:, n + 1, cols], in1=res[:, n, cols], op=ALU.add)
 
         def store(tiles, cols):
             nc.sync.dma_start(out=out_tiles[:, tiles, cols], in_=res[:, tiles, cols])
@@ -199,22 +199,28 @@ def tile_mix_glu48_fm_res_kernel(tc, x, w4_words, w4_scales, w8_words, w8_scales
         nc.vector.tensor_copy(out=w8_rows[64:P, 0, :].bitcast(I32), in_=w8_rows[0:64, 1, :].bitcast(I32))
 
         added = 0
-        for n in range(TILES - 1):
-            acc = up_product(n, whole)
-            if n + 1 in late:
+        for n in range(TILES - 2):
+            if n in late:
                 for a in range(PASSES):
-                    gate_pass(n + 1, a, whole)
-            parts = halves if n == TILES - 2 else [whole]
-            for cols in parts:
-                multiply(n, acc, cols)
-            ready = range(added, min(n + 1, POOL_TILES + ADDS_PER_TILE * max(0, n + 2 - BANKS)))
-            added = ready.stop
-            for m in ready:
-                for cols in parts:
-                    add(m, cols)
+                    gate_pass(n, a, whole)
+            multiply(n, up_product(n, whole), whole)
+            for m in range(added, ADDED_AFTER.get(n, added)):
+                add(m, whole)
                 if m + 1 in OUT_EDGES:
                     store(slice(OUT_EDGES[OUT_EDGES.index(m + 1) - 1], m + 1), whole)
+            added = ADDED_AFTER.get(n, added)
 
+        n = TILES - 2
+        for a in range(PASSES):
+            gate_pass(n, a, whole)
+        acc = up_product(n, whole)
+        for a in range(PASSES):
+            gate_pass(n + 1, a, whole)
+        for cols in halves:
+            multiply(n, acc, cols)
+        for cols in halves:
+            add(n, cols)
+        store(slice(OUT_EDGES[-2], n + 1), whole)
         last = TILES - 1
         parts = [halves[0], slice(HALF, HALF + P), slice(HALF + P, T)]
         sums = [up_product(last, cols) for cols in parts]

from contextlib import ExitStack

import concourse.mybir as mybir

K, M, T = 1536, 1536, 512
FLOPS = 2 * 2 * K * M * T

F32 = mybir.dt.float32
BF16 = mybir.dt.bfloat16
I32 = mybir.dt.int32
U32 = mybir.dt.uint32
U8 = mybir.dt.uint8
FP8X4 = mybir.dt.float8_e4m3fn_x4
FP4X4 = mybir.dt.float4_e2m1fn_x4
SILU = mybir.ActivationFunctionType.Silu
ALU = mybir.AluOpType

P = 128
PACK = 4
PASSES = K // (P * PACK)
TILES = M // P
BANKS = 8
ALIGN = 256
HALF = T // 2
W8_ROW = 4
VECTOR_CAST = 160
W8_EDGES = (0, 2, 5, 8, 10, TILES)
R_EDGES = (0, 3, 6, 9, TILES)
OUT_EDGES = (0, 4, 6, 8, 10, 11)
POOL_TILES = (0, 1, 2, 3)
ADDED_AFTER = {0: 1, 1: 2, 2: 3, 3: 4, 7: 6, 8: 8, 9: 10}


def tile_mix_glu48_fm_res_kernel(tc, x, w4_words, w4_scales, w8_words, w8_scales, r, out):
    nc = tc.nc
    whole = slice(0, T)
    halves = [slice(0, HALF), slice(HALF, T)]
    last_pass = PASSES - 1
    head = range(BANKS)
    late = range(BANKS, TILES)
    with ExitStack() as ctx:
        keep = ctx.enter_context(tc.tile_pool(name="keep", bufs=1))
        psum = ctx.enter_context(tc.psum_pool(name="psum", bufs=BANKS))
        ctx.enter_context(tc.manual_schedule())

        def sbuf(shape, dtype, name):
            return keep.tile(shape, dtype, name=name, tag=name, align_bytes=ALIGN)

        w4_planes = sbuf([P, PASSES, M], U8, "w4_planes")
        w8_rows = sbuf([P, 2, M], U8, "w8_rows")
        w8_planes = w8_rows[:, 0, :]
        table_in = sbuf([P, 8], F32, "table_in")
        table_out = sbuf([P, 8], F32, "table_out")
        nc.vector.memset(w4_planes[:].rearrange("p a n -> p (a n)").bitcast(I32), 0)
        nc.vector.memset(table_in[:], 0.0)
        nc.vector.memset(w8_rows[0:64].rearrange("p s n -> p (s n)").bitcast(I32), 0)
        nc.scalar.activation(out=table_out[:], in_=table_in[:], func=SILU)

        res = sbuf([P, TILES, T], F32, "res")
        slots = sbuf([P, TILES + 1, T], F32, "slots")
        raw = {}
        r_tiles = r.rearrange("(n p) t -> p n t", p=P)
        out_tiles = out.rearrange("(n p) t -> p n t", p=P)
        x_rows = x.rearrange("(a p j) t -> a p j t", p=P, j=PACK)
        w4_hbm = w4_words.rearrange("a p b -> p a b")
        w8_hbm = w8_words.rearrange("a p n i -> p a (n i)")
        w4 = {}
        w8 = {}

        def load_x(a, cols):
            block = sbuf([P, PACK, cols.stop - cols.start], F32, "raw_%d_%d" % (a, cols.start))
            nc.sync.dma_start(out=block[:], in_=x_rows[a][:, :, cols])
            for half in halves:
                if cols.start <= half.start < cols.stop:
                    raw[a, half.start] = block[:, :, half.start - cols.start : half.stop - cols.start]

        def load_w4_planes():
            rows = w4_scales.rearrange("a (q i) n -> i q a n", i=4)
            for i in range(4):
                nc.sync.dma_start(out=w4_planes[i:P:32, :, :].bitcast(I32), in_=rows[i].bitcast(I32))

        def load_w8_planes():
            for q in range(4):
                nc.sync.dma_start(
                    out=w8_rows[32 * (q % 2) : 32 * (q % 2) + W8_ROW * PASSES, q // 2, :].bitcast(I32),
                    in_=w8_scales[:, 4 * q : 4 * q + 4, :].bitcast(I32),
                )

        def load_w4(passes, tiles):
            block = sbuf([P, len(passes), 2 * P * len(tiles)], U8, "w4_%d_%d" % (passes.start, tiles.start))
            source = w4_hbm[:, passes.start : passes.stop, 2 * P * tiles.start : 2 * P * tiles.stop]
            nc.sync.dma_start(out=block[:].bitcast(I32), in_=source.bitcast(I32))
            for i, a in enumerate(passes):
                for j, n in enumerate(tiles):
                    w4[n, a] = block[:, i, 2 * P * j : 2 * P * (j + 1)]

        def load_w8(b):
            tiles = range(W8_EDGES[b], W8_EDGES[b + 1])
            block = sbuf([P, PASSES, P * len(tiles)], U32, "w8_%d" % b)
            source = w8_hbm[:, :, 4 * P * tiles.start : 4 * P * tiles.stop]
            nc.sync.dma_start(out=block[:].bitcast(I32), in_=source.bitcast(I32))
            for j, n in enumerate(tiles):
                for a in range(PASSES):
                    w8[n, a] = block[:, a, P * j : P * (j + 1)]

        def load_r(c):
            tiles = slice(R_EDGES[c], R_EDGES[c + 1])
            nc.sync.dma_start(out=res[:, tiles, :], in_=r_tiles[:, tiles, :])

        load_x(0, halves[0])
        load_w4(range(0, 1), head)
        load_w4_planes()
        load_x(0, halves[1])
        load_x(1, whole)
        load_w4(range(1, 3), head)
        load_x(2, halves[0])
        load_x(2, halves[1])
        load_w8_planes()
        load_w8(0)
        load_w8(1)
        load_r(0)
        load_w8(2)
        load_r(1)
        load_w4(range(PASSES), late)
        load_w8(3)
        load_r(2)
        load_w8(4)
        load_r(3)

        x_codes = [sbuf([P, T], U32, "x_codes_%d" % a) for a in range(PASSES)]
        x_scales = [sbuf([P, T], U8, "x_scales_%d" % a) for a in range(PASSES)]
        grouped = [sbuf([P, T, PACK], BF16, "grouped_%d" % a) for a in range(PASSES)]

        def cast(engine_copy, a, half, share):
            dst = grouped[a][:, half, :][:, share, :].rearrange("p (c i) j -> p c j i", i=4)
            src = raw[a, half.start][:, :, share].rearrange("p j (c i) -> p c j i", i=4)
            engine_copy(out=dst, in_=src)

        def quantize(a, cols):
            nc.vector.quantize_mx(
                out=x_codes[a][:, cols].bitcast(FP8X4),
                scales=x_scales[a][:, cols],
                in_=grouped[a][:, cols, :].rearrange("p t j -> p (t j)"),
            )

        gate = {}
        act = {}

        def gate_pass(n, a, cols):
            if n not in gate:
                gate[n] = psum.tile([P, T], F32, name="acc", tag="acc")
            closing = a == last_pass and cols.stop == T
            nc.tensor.matmul_mx(
                out=gate[n][:, cols],
                lhsT=w4[n, a].bitcast(FP4X4),
                lhsT_scale=w4_planes[:, a, n * P : (n + 1) * P],
                rhs=x_codes[a][:, cols].bitcast(FP8X4),
                rhs_scale=x_scales[a][:, cols],
                start=(a == 0 and cols.start == 0),
                stop=closing,
            )
            if closing:
                act[n] = sbuf([P, T], F32, "act_%d" % n)
                for part in halves if n == TILES - 1 else [whole]:
                    nc.scalar.activation(out=act[n][:, part], in_=gate[n][:, part], func=SILU)

        def up_product(n, cols):
            acc = psum.tile([P, T], F32, name="acc", tag="acc")
            for a in range(PASSES):
                nc.tensor.matmul_mx(
                    out=acc[:, cols],
                    lhsT=w8[n, a].bitcast(FP8X4),
                    lhsT_scale=w8_planes[W8_ROW * a : P, n * P : (n + 1) * P],
                    rhs=x_codes[a][:, cols].bitcast(FP8X4),
                    rhs_scale=x_scales[a][:, cols],
                    start=(a == 0),
                    stop=(a == last_pass),
                )
            return acc

        def multiply(n, acc, cols):
            nc.vector.tensor_tensor(out=slots[:, n + 1, cols], in0=acc[:, cols], in1=act[n][:, cols], op=ALU.mult)

        def add(n, cols):
            engine = nc.gpsimd if n in POOL_TILES else nc.vector
            engine.tensor_tensor(out=res[:, n, cols], in0=slots[:, n + 1, cols], in1=res[:, n, cols], op=ALU.add)

        def store(tiles, cols):
            nc.sync.dma_start(out=out_tiles[:, tiles, cols], in_=res[:, tiles, cols])

        for a in range(PASSES):
            for half in halves:
                cast(nc.vector.tensor_copy, a, half, slice(0, VECTOR_CAST))
                cast(nc.scalar.copy, a, half, slice(VECTOR_CAST, HALF))
                quantize(a, half)
                for n in head:
                    gate_pass(n, a, half)

        nc.vector.tensor_copy(out=w8_rows[64:P, 0, :].bitcast(I32), in_=w8_rows[0:64, 1, :].bitcast(I32))

        added = 0
        for n in range(TILES - 2):
            if n in late:
                for a in range(PASSES):
                    gate_pass(n, a, whole)
            multiply(n, up_product(n, whole), whole)
            for m in range(added, ADDED_AFTER.get(n, added)):
                add(m, whole)
                if m + 1 in OUT_EDGES:
                    store(slice(OUT_EDGES[OUT_EDGES.index(m + 1) - 1], m + 1), whole)
            added = ADDED_AFTER.get(n, added)

        n = TILES - 2
        for a in range(PASSES):
            gate_pass(n, a, whole)
        acc = up_product(n, whole)
        for a in range(PASSES):
            gate_pass(n + 1, a, whole)
        for cols in halves:
            multiply(n, acc, cols)
        for cols in halves:
            add(n, cols)
        store(slice(OUT_EDGES[-2], n + 1), whole)
        last = TILES - 1
        parts = [halves[0], slice(HALF, HALF + P), slice(HALF + P, T)]
        sums = [up_product(last, cols) for cols in parts]
        for acc, cols in zip(sums, parts):
            multiply(last, acc, cols)
        add(last, parts[0])
        store(slice(last, TILES), halves[0])
        add(last, parts[1])
        add(last, parts[2])
        store(slice(last, TILES), halves[1])
